import numpy as np
import ml_dtypes


def mxq(x, axis, fmt="e4m3"):
    dtype, down = {"e4m3": (ml_dtypes.float8_e4m3fn, 7), "e5m2": (ml_dtypes.float8_e5m2, 14)}[fmt]
    v = np.moveaxis(np.asarray(x, np.float32).astype(ml_dtypes.bfloat16).astype(np.float64), axis, -1)
    blocks = v.reshape(v.shape[:-1] + (-1, 32))
    amax = np.abs(blocks).max(-1, keepdims=True)
    byte = np.maximum(np.where(amax > 0, np.frexp(amax)[1] - 1 + 127, 0) - down, 1)
    scale = np.exp2(byte - 127.0)
    codes = (blocks / scale).astype(np.float32).astype(dtype).astype(np.float64)
    return np.moveaxis((codes * scale).reshape(v.shape), -1, axis)


WIDE = False


def mx_kscale(k):
    if not WIDE:
        return np.ones(k)
    levels = np.array([10, -10, 5, -5, 0])
    if k % 512:
        return np.exp2(np.random.permutation(np.resize(levels, k // 32))).repeat(32)
    a = np.empty((k // 512, 16))
    for p in range(k // 512):
        a[p, :8] = np.random.permutation(np.resize(levels, 8))
        for g in range(8):
            far = levels[np.abs(levels - a[p, g]) >= 10]
            a[p, g + 8] = far[np.random.randint(len(far))]
    return np.exp2(a.ravel()).repeat(32)


BF16 = ml_dtypes.bfloat16


def bf(x):
    return np.asarray(x, np.float32).astype(BF16)


def f64(x):
    return np.asarray(x).astype(np.float64)


E2M1 = np.array([0.0, 0.5, 1.0, 1.5, 2.0, 3.0, 4.0, 6.0, -0.0, -0.5, -1.0, -1.5, -2.0, -3.0, -4.0, -6.0])


def pack_weight(w, fmt):
    k, n = w.shape
    w = f64(bf(w)).reshape(k // 32, 32, n)
    amax = np.abs(w).max(1)
    if fmt == "e4m3":
        byte = np.frexp(amax)[1] - 1 + 127 - 7
    else:
        mant, ex = np.frexp(amax / 6.0)
        byte = np.where(mant > 0.5, ex, ex - 1) + 127
    byte = np.clip(np.where(amax > 0, byte, 1), 1, 254)
    scaled = (w * np.exp2(127.0 - byte)[:, None, :]).reshape(k, n).astype(np.float32)
    by_word = np.ascontiguousarray(scaled.reshape(k // 512, 128, 4, n).transpose(0, 1, 3, 2))
    if fmt == "e4m3":
        words = by_word.astype(ml_dtypes.float8_e4m3fn).view(np.uint8)
    else:
        c = by_word.astype(ml_dtypes.float4_e2m1fn).view(np.uint8) & 0xF
        words = c[..., 0::2] | (c[..., 1::2] << 4)
    return np.ascontiguousarray(words), np.ascontiguousarray(byte.astype(np.uint8).reshape(k // 512, 16, n))


def unpack_weight(words, scales, fmt):
    g, p, n, _ = words.shape
    if fmt == "e4m3":
        vals = np.ascontiguousarray(words).view(ml_dtypes.float8_e4m3fn).astype(np.float64)
    else:
        nib = np.empty((g, p, n, 4), np.uint8)
        nib[..., 0::2] = words & 0xF
        nib[..., 1::2] = words >> 4
        vals = E2M1[nib]
    vals = vals * np.repeat(np.exp2(scales.astype(np.float64) - 127.0), 8, axis=1)[..., None]
    return vals.transpose(0, 1, 3, 2).reshape(g * 512, n)
def pack4(w):
    words, scales = pack_weight(w, "e2m1")
    return words.reshape(words.shape[0], 128, -1), scales


def unpack4(words, scales):
    return unpack_weight(words.reshape(words.shape[0], 128, -1, 2), scales, "e2m1")


P, Q, TA, TB, L = 512, 512, 2048, 1024, 2048


def setup_inputs():
    s, r, t = mx_kscale(TA), mx_kscale(TB), mx_kscale(L)
    c = L ** 0.25
    overlap = np.abs(np.random.standard_normal((TA, L))) / np.sqrt(TA)
    ovl_words, ovl_scales = pack4(overlap / s[:, None])
    return {"ra": bf(np.random.standard_normal((P, TA)) * s),
            "ovl_words": ovl_words,
            "ovl_scales": ovl_scales,
            "wt": bf(np.random.uniform(0.5, 1.5, L) / c * t),
            "yb": bf(np.random.standard_normal((Q, TB)) * r),
            "diff": bf(np.random.standard_normal((TB, L)) / np.sqrt(TB) / c / r[:, None] / t),
            "lo": bf(-np.random.uniform(1.0, 1.5, L) / c / t),
            "hi": bf(np.random.uniform(1.0, 1.5, L) / c / t)}


def reference(ra, ovl_words, ovl_scales, wt, yb, diff, lo, hi):
    u = mxq(f64(ra), 1, "e4m3") @ unpack4(ovl_words, ovl_scales)
    u = u * f64(wt)
    v = mxq(f64(yb), 1, "e4m3") @ mxq(f64(diff), 0, "e4m3")
    v = np.minimum(np.maximum(v, f64(lo)), f64(hi))
    return mxq(u, 1, "e4m3") @ mxq(v, 1, "e4m3").T

@@ -1,0 +1,416 @@
+from contextlib import ExitStack
+
+import concourse.mybir as mybir
+from concourse.masks import make_identity
+
+ASSETS, TA, TB, L = 512, 2048, 1024, 2048
+FLOPS = 2 * ASSETS * (TA * L + TB * L + L * ASSETS)
+
+F32 = mybir.dt.float32
+BF16 = mybir.dt.bfloat16
+I32 = mybir.dt.int32
+U8 = mybir.dt.uint8
+FP8X4 = mybir.dt.float8_e4m3fn_x4
+FP4X4 = mybir.dt.float4_e2m1fn_x4
+ALU = mybir.AluOpType
+ACT = mybir.ActivationFunctionType
+
+P = 128
+PACK = 4
+K_PASS = P * PACK
+RA_PASSES, YB_PASSES, GROUPS = TA // K_PASS, TB // K_PASS, L // K_PASS
+TILES = ASSETS // P
+
+
+def tile_clipped_overlap_covariance_s11_kernel(tc, ra, ovl_words, ovl_scales, wt, yb, diff, lo, hi, out):
+    nc = tc.nc
+    with ExitStack() as ctx:
+        sb = ctx.enter_context(tc.tile_pool(name="sb", bufs=1))
+        psum = ctx.enter_context(tc.psum_pool(name="psum", bufs=1))
+        ctx.enter_context(tc.manual_schedule())
+
+        def copy_on(engine, dst, src):
+            if engine == "scalar":
+                nc.scalar.copy(out=dst, in_=src)
+            else:
+                nc.vector.tensor_copy(out=dst, in_=src)
+
+        turn = [0, list(range(8))]
+
+        def new_bank(n=None):
+            if n is None:
+                n = turn[1][turn[0] % len(turn[1])]
+                turn[0] = turn[0] + 1
+            return psum.tile([P, K_PASS], F32, name="bank%d" % n)
+
+        def new_packed():
+            return sb.tile([P, K_PASS * PACK], BF16, name="packed", bufs=8, align_bytes=64)
+
+        def quantise(packed, name, c0=0, c1=K_PASS, into=None):
+            if into is None:
+                codes = sb.tile([P, K_PASS], I32, name=name + "_codes", align_bytes=64)
+                scales = sb.tile([P, K_PASS], U8, name=name + "_scales", align_bytes=64)
+                into = (codes, scales)
+            nc.vector.quantize_mx(out=into[0][:, c0:c1].bitcast(FP8X4), scales=into[1][:, c0:c1], in_=packed[:, PACK * c0 : PACK * c1])
+            return into
+
+        def load_ticks(src, g, name):
+            rows = sb.tile([P, TILES, K_PASS], BF16, name="%s_rows%d" % (name, g))
+            nc.sync.dma_start(out=rows[:], in_=src[:, g * K_PASS : (g + 1) * K_PASS].rearrange("(a p) k -> p a k", p=P))
+            return rows
+
+        def turn_ticks(rows, engines=("scalar", "scalar")):
+            packed = new_packed()
+            words = rows[:].bitcast(F32)
+            for half in range(2):
+                bank = new_bank()
+                for a in range(2):
+                    for u in range(2):
+                        c = (2 * a + u) * P
+                        nc.tensor.transpose(bank[:, c : c + P], words[:, 2 * half + a, u : 2 * P : 2], ident[:])
+                copy_on(
+                    engines[half],
+                    packed[:].bitcast(F32)[:, half * K_PASS : (half + 1) * K_PASS].rearrange("p (a i u) -> p a i u", a=2, u=2),
+                    bank[:].rearrange("p (a u i) -> p a i u", a=2, u=2),
+                )
+            return packed
+
+        def turn_half(words, packed, half, engine):
+            bank = new_bank()
+            for a in range(2):
+                for u in range(2):
+                    c = (2 * a + u) * P
+                    nc.tensor.transpose(bank[:, c : c + P], words[:, a, u : 2 * P : 2], ident[:])
+            copy_on(
+                engine,
+                packed[:].bitcast(F32)[:, half * K_PASS : (half + 1) * K_PASS].rearrange("p (a i u) -> p a i u", a=2, u=2),
+                bank[:].rearrange("p (a u i) -> p a i u", a=2, u=2),
+            )
+
+        def pack_diff_part(rows, packed, t0, t1, engine):
+            copy_on(
+                engine,
+                packed[:].rearrange("p (t q r j) -> p q t j r", t=PACK, r=8, j=PACK)[:, :, t0:t1],
+                rows.rearrange("p j (q t r) -> p q t j r", t=PACK, r=8)[:, :, t0:t1],
+            )
+
+        def load_diff(grp, g):
+            rows = sb.tile([P, PACK, K_PASS], BF16, name="diff_rows%d_%d" % (grp, g))
+            src = diff[g * K_PASS : (g + 1) * K_PASS, grp * K_PASS : (grp + 1) * K_PASS]
+            nc.sync.dma_start(out=rows[:], in_=src.rearrange("(p j) l -> p j l", j=PACK))
+            return rows
+
+        def pack_diff(rows, engine):
+            packed = new_packed()
+            copy_on(
+                engine,
+                packed[:].rearrange("p (t q r j) -> p q t j r", t=PACK, r=8, j=PACK),
+                rows[:].rearrange("p j (q t r) -> p q t j r", t=PACK, r=8),
+            )
+            return packed
+
+        def load_ovl(grp):
+            words = sb.tile([P, RA_PASSES, K_PASS // 2], I32, name="ovl_rows%d" % grp)
+            src = ovl_words.bitcast(I32)[:, :, grp * K_PASS // 2 : (grp + 1) * K_PASS // 2]
+            nc.sync.dma_start(out=words[:], in_=src.rearrange("g p w -> p g w"))
+            return words
+
+        def load_ovl_scales(plane, first_word, words):
+            src = ovl_scales.bitcast(I32)[:, :, first_word : first_word + words]
+            for r in range(4):
+                nc.sync.dma_start(out=plane[r:P:32, :, :], in_=src[:, r:16:4, :].rearrange("g q w -> q g w"))
+
+        def sort_ovl(grp, words, plane):
+            codes = sb.tile([P, RA_PASSES, K_PASS // 2], I32, name="ovl_codes%d" % grp, align_bytes=64)
+            scales = sb.tile([P, RA_PASSES, K_PASS // 4], I32, name="ovl_scales%d" % grp, align_bytes=64)
+            nc.vector.tensor_copy(
+                out=codes[:].rearrange("p g (t q w) -> p g t q w", t=PACK, w=4),
+                in_=words[:].rearrange("p g (q t w) -> p g t q w", t=PACK, w=4),
+            )
+            nc.vector.tensor_copy(
+                out=scales[:].rearrange("p g (t q w) -> p g t q w", t=PACK, w=2),
+                in_=plane.rearrange("p g (q t w) -> p g t q w", t=PACK, w=2),
+            )
+            return codes, scales
+
+        def sort_codes(grp, words):
+            codes = sb.tile([P, RA_PASSES, K_PASS // 2], I32, name="ovl_codes%d" % grp, align_bytes=64)
+            nc.vector.tensor_copy(
+                out=codes[:].rearrange("p g (t q w) -> p g t q w", t=PACK, w=4),
+                in_=words[:].rearrange("p g (q t w) -> p g t q w", t=PACK, w=4),
+            )
+            return codes
+
+        def sort_scales(grp, plane):
+            scales = sb.tile([P, RA_PASSES, K_PASS // 4], I32, name="ovl_scales%d" % grp, align_bytes=64)
+            nc.vector.tensor_copy(
+                out=scales[:].rearrange("p g (t q w) -> p g t q w", t=PACK, w=2),
+                in_=plane.rearrange("p g (q t w) -> p g t q w", t=PACK, w=2),
+            )
+            return scales
+
+        def u_pass(bank, ovl_mx, t, g, ra_g):
+            nc.tensor.matmul_mx(
+                out=bank[:],
+                lhsT=ovl_mx[0][:, g, t * P // 2 : (t + 1) * P // 2].bitcast(FP4X4),
+                lhsT_scale=ovl_mx[1][:, g, t * P // 4 : (t + 1) * P // 4].bitcast(U8),
+                rhs=ra_g[0][:].bitcast(FP8X4),
+                rhs_scale=ra_g[1][:],
+                start=(g == 0),
+                stop=(g == RA_PASSES - 1),
+            )
+
+        def v_pass(bank, diff_g, t, g, yb_g):
+            nc.tensor.matmul_mx(
+                out=bank[:],
+                lhsT=diff_g[0][:, t * P : (t + 1) * P].bitcast(FP8X4),
+                lhsT_scale=diff_g[1][:, t * P : (t + 1) * P],
+                rhs=yb_g[0][:].bitcast(FP8X4),
+                rhs_scale=yb_g[1][:],
+                start=(g == 0),
+                stop=(g == YB_PASSES - 1),
+            )
+
+        def new_slots():
+            return sb.tile([P, PACK, ASSETS], BF16, name="slots", bufs=8)
+
+        def weigh(bank, slots, grp, t):
+            nc.scalar.activation(out=slots[:, t, :], in_=bank[:], func=ACT.Copy, scale=consts[:, t, grp : grp + 1])
+
+        def clip(bank, slots, grp, t):
+            nc.vector.tensor_scalar(
+                out=slots[:, t, :],
+                in0=bank[:],
+                scalar1=consts[:, t, GROUPS + grp : GROUPS + grp + 1],
+                scalar2=consts[:, t, 2 * GROUPS + grp : 2 * GROUPS + grp + 1],
+                op0=ALU.max,
+                op1=ALU.min,
+            )
+
+        def pack_slots(slots, engine, packed=None, c0=0, c1=ASSETS):
+            if packed is None:
+                packed = new_packed()
+            copy_on(
+                engine,
+                packed[:, PACK * c0 : PACK * c1].rearrange("p (c i t) -> p c t i", i=4, t=PACK),
+                slots[:, :, c0:c1].rearrange("p t (c i) -> p c t i", i=4),
+            )
+            return packed
+
+        def v_group(grp, diff_mx):
+            slots = new_slots()
+            for t in range(PACK):
+                bank = new_bank()
+                for g in range(YB_PASSES):
+                    v_pass(bank, diff_mx[g], t, g, yb_mx[g])
+                clip(bank, slots, grp, t)
+            return slots
+
+        def u_slot(grp, ovl_mx, slots, t):
+            bank = new_bank()
+            for g in range(RA_PASSES):
+                u_pass(bank, ovl_mx, t, g, ra_mx[g])
+            weigh(bank, slots, grp, t)
+
+        def out_pass(bank, a, grp):
+            nc.tensor.matmul_mx(
+                out=bank[:],
+                lhsT=u_mx[grp][0][:, a * P : (a + 1) * P].bitcast(FP8X4),
+                lhsT_scale=u_mx[grp][1][:, a * P : (a + 1) * P],
+                rhs=v_mx[grp][0][:].bitcast(FP8X4),
+                rhs_scale=v_mx[grp][1][:],
+                start=(grp == 0),
+                stop=(grp == GROUPS - 1),
+            )
+
+        def store(bank, a, engine):
+            res = sb.tile([P, ASSETS], F32, name="res%d" % a)
+            copy_on(engine, res[:], bank[:])
+            nc.sync.dma_start(out=out[a * P : (a + 1) * P, :], in_=res[:])
+
+        ident = sb.tile([P, P], F32, name="ident")
+        make_identity(nc, ident[:])
+        const_sorted = sb.tile([P, K_PASS], F32, name="const_sorted")
+        nc.gpsimd.memset(const_sorted[:], 0.0)
+        warm_in = sb.tile([P, K_PASS], BF16, name="warm_in", align_bytes=64)
+        warm_codes = sb.tile([P, P], I32, name="warm_codes", align_bytes=64)
+        warm_scales = sb.tile([P, P], U8, name="warm_scales", align_bytes=64)
+        nc.vector.memset(warm_in[:], 1.0)
+        nc.vector.quantize_mx(out=warm_codes[:].bitcast(FP8X4), scales=warm_scales[:], in_=warm_in[:])
+
+        def warm(count):
+            bank = new_bank(3)
+            for i in range(count):
+                nc.tensor.matmul_mx(out=bank[:, 0:P], lhsT=warm_codes[:].bitcast(FP8X4), lhsT_scale=warm_scales[:], rhs=warm_codes[:].bitcast(FP8X4), rhs_scale=warm_scales[:], start=True, stop=True)
+
+        plane_first = sb.tile([P, RA_PASSES, K_PASS // 4], I32, name="plane_first")
+        plane_second = sb.tile([P, RA_PASSES, K_PASS // 4], I32, name="plane_second")
+        plane_rest = sb.tile([P, RA_PASSES, (L - 2 * K_PASS) // 4], I32, name="plane_rest")
+        nc.vector.memset(plane_first[:], 0)
+        nc.vector.memset(plane_second[:], 0)
+        nc.vector.memset(plane_rest[:], 0)
+        planes = [plane_first[:], plane_second[:]] + [plane_rest[:, :, i * K_PASS // 4 : (i + 1) * K_PASS // 4] for i in range(GROUPS - 2)]
+        const_rows = sb.tile([P, K_PASS], BF16, name="const_rows")
+        consts = sb.tile([P, PACK, 3 * GROUPS], F32, name="consts")
+
+        def load_consts():
+            for n, vec in enumerate((wt, lo, hi)):
+                nc.sync.dma_start(out=const_rows[n * GROUPS : (n + 1) * GROUPS, :], in_=vec.rearrange("(g l) -> g l", g=GROUPS))
+
+        live = 3 * GROUPS
+
+        def sort_consts():
+            nc.vector.tensor_copy(
+                out=const_sorted[0:live, :].rearrange("p (t q r) -> p t q r", t=PACK, r=8),
+                in_=const_rows[0:live, :].rearrange("p (q t r) -> p t q r", t=PACK, r=8),
+            )
+
+        def turn_consts():
+            bank = new_bank()
+            for t in range(PACK):
+                nc.tensor.transpose(bank[:, t * P : (t + 1) * P], const_sorted[:, t * P : (t + 1) * P], ident[:])
+            nc.scalar.copy(out=consts[:], in_=bank[:].rearrange("p (t c) -> p t c", t=PACK)[:, :, 0:live])
+
+        tick_words, diff_rows, ovl_rows = {}, {}, {}
+        for item in "Y00 Y01 d00 r0 c d01 r1 s0 o0 r2 r3 d10 d11 s1 o1 d20 d21 s2 o2 d30 d31 o3".split():
+            n = [int(c) for c in item if c in "0123456789"]
+            if item[0] in "yr":
+                rows = load_ticks(yb if item[0] == "y" else ra, n[0], item[0])
+                for h in range(2):
+                    tick_words[item[0], n[0], h] = rows[:].bitcast(F32)[:, 2 * h : 2 * h + 2, :]
+            elif item[0] in "YR":
+                src = yb if item[0] == "Y" else ra
+                rows = sb.tile([P, 2, 2 * K_PASS], BF16, name=item)
+                nc.sync.dma_start(out=rows[:], in_=src[n[1] * 2 * P : (n[1] + 1) * 2 * P, n[0] * 2 * K_PASS : (n[0] + 1) * 2 * K_PASS].rearrange("(a p) k -> p a k", p=P))
+                for g in range(2):
+                    tick_words["y" if item[0] == "Y" else "r", 2 * n[0] + g, n[1]] = rows[:].bitcast(F32)[:, :, g * 2 * P : (g + 1) * 2 * P]
+            elif item[0] == "d":
+                diff_rows[n[0], n[1]] = load_diff(n[0], n[1])[:]
+            elif item[0] == "D":
+                rows = sb.tile([P, PACK, 2 * K_PASS], BF16, name=item)
+                src = diff[n[1] * K_PASS : (n[1] + 1) * K_PASS, n[0] * 2 * K_PASS : (n[0] + 1) * 2 * K_PASS]
+                nc.sync.dma_start(out=rows[:], in_=src.rearrange("(p j) l -> p j l", j=PACK))
+                for i in range(2):
+                    diff_rows[2 * n[0] + i, n[1]] = rows[:, :, i * K_PASS : (i + 1) * K_PASS]
+            elif item[0] == "o":
+                ovl_rows[n[0]] = load_ovl(n[0])
+            elif item == "c":
+                load_consts()
+            elif item == "s0":
+                load_ovl_scales(plane_first, 0, K_PASS // 4)
+            elif item == "s1":
+                load_ovl_scales(plane_second, K_PASS // 4, K_PASS // 4)
+            else:
+                load_ovl_scales(plane_rest, K_PASS // 2, (L - 2 * K_PASS) // 4)
+
+        on_scalar = "Id011 Iv00 Iv01 Id111 Id20 Iv1 Id30 Iv2 Iu2 Iv31 Iu330 E0 E2".split()
+        yb_mx, ra_mx, u_mx, v_mx, diff_mx, ovl_mx, packs, held, slots = {}, {}, {}, {}, {}, {}, {}, {}, {}
+        last = GROUPS - 1
+        banks, sorted_scales = {}, {}
+        for item in """W18 use4567 Ty00 Ty10 Ty01 Ty11 W8 Id00 Qy0 Tr00 Tr01 Qd00 Qy1 Sk Vp000 Id010 Id011 Tc Qr0 Qd01 Tr10 Tr11 Vp01 Ss0 Sc0 C00 C01 Qr1 C02 C03
+ Tr20 Tr21 Up000 Iv00 Qr2 Id10 Tr30 Tr31 Up01 Up02 Id110 Id111 Qr3 Qd10 Up03 Qd11 Iv01 Ss1 Sc1 M00 M01 use45670123 M02 M03 Vs10 C10 Vs11 C11 Vs12 C12 Vs13 C13 Id20 Id21 Qv0 Qd20 Us10 M10 Us11 M11 Qd21 Ss2 Sc2 Iv1 Iu0 Us12 Us13 Qu0 M12 M13 Vs20 C20 Vs21 C21 Vs22 C22 Vs23 C23 Id30 Id31 Qv1 Qd30 Us20 M20 Us21 M21 Qd31 Ss3 Sc3 Iv2 Iu1 Us22 Us23 Qu1 M22 M23 Vs30 C30 Vs31 C31 Vs32 C32 Vs33 C33 Iu2 Qv2 Us30 M30 Us31 M31 Iv30 Iv31 Us32 M32 Us33 M33 Qu2 Qv3 O00 O10 O20 O30 O01 O11 O21 O31 O02 O12 O22 O32 Iu300 Iu310 Qu30 Iu330 Iu320 Qu31 Qu32 Qu33 O03 E0 O13 E1 O23 E2 O33 E3""".split():
+            engine = "scalar" if item in on_scalar else "vector"
+            n = [int(c) for c in item if c in "0123456789"]
+            kind = "".join([c for c in item if c not in "0123456789"])
+            if kind == "Ty" or kind == "Tr":
+                key = item[1:3]
+                if key not in packs:
+                    packs[key] = new_packed()
+                turn_half(tick_words[item[1], n[0], n[1]], packs[key], n[1], "vector" if item in on_scalar else "scalar")
+            elif kind == "Tc":
+                turn_consts()
+            elif kind == "Id":
+                key = item[1:4]
+                if key not in packs:
+                    packs[key] = new_packed()
+                if len(n) == 2:
+                    pack_diff_part(diff_rows[n[0], n[1]], packs[key], 0, 4, engine)
+                else:
+                    pack_diff_part(diff_rows[n[0], n[1]], packs[key], 2 * n[2], 2 * n[2] + 2, engine)
+            elif kind == "Iu" or kind == "Iv":
+                key = item[1:3]
+                if key not in packs:
+                    packs[key] = new_packed()
+                if len(n) == 1:
+                    pack_slots(slots[key], engine, packs[key])
+                elif len(n) == 2:
+                    pack_slots(slots[key], engine, packs[key], 2 * P * n[1], 2 * P * (n[1] + 1))
+                else:
+                    pack_slots(slots[key], engine, packs[key], P * n[1], P * (n[1] + 1))
+            elif kind == "Qy":
+                yb_mx[n[0]] = quantise(packs[item[1:]], item)
+            elif kind == "Qr":
+                ra_mx[n[0]] = quantise(packs[item[1:]], item)
+            elif kind == "Qd":
+                diff_mx[n[0], n[1]] = quantise(packs[item[1:]], item)
+            elif kind == "Qu" and len(n) == 1:
+                u_mx[n[0]] = quantise(packs[item[1:]], item)
+            elif kind == "Qu":
+                u_mx[n[0]] = quantise(packs[item[1:3]], item[0:3], n[1] * P, (n[1] + 1) * P, u_mx.get(n[0]))
+            elif kind == "Qv":
+                v_mx[n[0]] = quantise(packs[item[1:]], item)
+            elif kind == "S":
+                ovl_mx[n[0]] = sort_ovl(n[0], ovl_rows[n[0]], planes[n[0]])
+            elif kind == "Sc":
+                ovl_mx[n[0]] = (sort_codes(n[0], ovl_rows[n[0]]), sorted_scales[n[0]])
+            elif kind == "Ss":
+                sorted_scales[n[0]] = sort_scales(n[0], planes[n[0]])
+            elif kind == "Sk":
+                sort_consts()
+            elif kind == "W":
+                warm(int(item[1:]))
+            elif kind == "Vp" or kind == "Up":
+                name = ("v" if kind == "Vp" else "u") + str(n[0])
+                if n[1] == 0:
+                    held[name] = [new_bank(n[2] + t) for t in range(PACK)]
+                for t in range(PACK):
+                    if kind == "Vp":
+                        v_pass(held[name][t], diff_mx[n[0], n[1]], t, n[1], yb_mx[n[1]])
+                    else:
+                        u_pass(held[name][t], ovl_mx[n[0]], t, n[1], ra_mx[n[1]])
+            elif kind == "Vs" or kind == "Us":
+                name = ("v" if kind == "Vs" else "u") + str(n[0])
+                bank = new_bank()
+                held.setdefault(name, []).append(bank)
+                if kind == "Vs":
+                    for g in range(YB_PASSES):
+                        v_pass(bank, diff_mx[n[0], g], n[1], g, yb_mx[g])
+                else:
+                    for g in range(RA_PASSES):
+                        u_pass(bank, ovl_mx[n[0]], n[1], g, ra_mx[g])
+            elif kind == "C" or kind == "M":
+                name = ("v" if kind == "C" else "u") + str(n[0])
+                if n[1] == 0:
+                    slots[name] = new_slots()
+                if kind == "C":
+                    clip(held[name][n[1]], slots[name], n[0], n[1])
+                else:
+                    weigh(held[name][n[1]], slots[name], n[0], n[1])
+            elif kind == "use":
+                turn[0], turn[1] = 0, n
+            elif kind == "Vg" or kind == "Ug":
+                name = ("v" if kind == "Vg" else "u") + str(n[0])
+                if n[1] == 0:
+                    held[name] = [new_bank(n[2] + t) for t in range(PACK)]
+                    slots[name] = new_slots()
+                for t in range(PACK):
+                    if kind == "Vg":
+                        v_pass(held[name][t], diff_mx[n[0], n[1]], t, n[1], yb_mx[n[1]])
+                        if n[1] == YB_PASSES - 1:
+                            clip(held[name][t], slots[name], n[0], t)
+                    else:
+                        u_pass(held[name][t], ovl_mx[n[0]], t, n[1], ra_mx[n[1]])
+                        if n[1] == RA_PASSES - 1:
+                            weigh(held[name][t], slots[name], n[0], t)
+            elif kind == "V":
+                slots["v%d" % n[0]] = v_group(n[0], [diff_mx[n[0], 0], diff_mx[n[0], 1]])
+            elif kind == "Ut":
+                if n[1] == 0:
+                    slots["u%d" % n[0]] = new_slots()
+                u_slot(n[0], ovl_mx[n[0]], slots["u%d" % n[0]], n[1])
+            elif kind == "O":
+                if n[1] == 0:
+                    banks[n[0]] = new_bank()
+                out_pass(banks[n[0]], n[0], n[1])
+            elif kind == "E":
+                store(banks[n[0]], n[0], engine)

@@ -174,8 +174,11 @@ def tile_clipped_overlap_covariance_s11_kernel(tc, ra, ovl_words, ovl_scales, wt
         def new_slots():
             return sb.tile([P, PACK, ASSETS], BF16, name="slots", bufs=8)
 
-        def weigh(bank, slots, grp, t):
-            nc.scalar.activation(out=slots[:, t, :], in_=bank[:], func=ACT.Copy, scale=consts[:, t, grp : grp + 1])
+        def weigh(bank, slots, grp, t, engine="scalar"):
+            if engine == "scalar":
+                nc.scalar.activation(out=slots[:, t, :], in_=bank[:], func=ACT.Copy, scale=consts[:, t, grp : grp + 1])
+            else:
+                nc.vector.tensor_scalar_mul(out=slots[:, t, :], in0=bank[:], scalar1=consts[:, t, grp : grp + 1])
 
         def clip(bank, slots, grp, t):
             nc.vector.tensor_scalar(
@@ -232,17 +235,6 @@ def tile_clipped_overlap_covariance_s11_kernel(tc, ra, ovl_words, ovl_scales, wt
         make_identity(nc, ident[:])
         const_sorted = sb.tile([P, K_PASS], F32, name="const_sorted")
         nc.gpsimd.memset(const_sorted[:], 0.0)
-        warm_in = sb.tile([P, K_PASS], BF16, name="warm_in", align_bytes=64)
-        warm_codes = sb.tile([P, P], I32, name="warm_codes", align_bytes=64)
-        warm_scales = sb.tile([P, P], U8, name="warm_scales", align_bytes=64)
-        nc.vector.memset(warm_in[:], 1.0)
-        nc.vector.quantize_mx(out=warm_codes[:].bitcast(FP8X4), scales=warm_scales[:], in_=warm_in[:])
-
-        def warm(count):
-            bank = new_bank(3)
-            for i in range(count):
-                nc.tensor.matmul_mx(out=bank[:, 0:P], lhsT=warm_codes[:].bitcast(FP8X4), lhsT_scale=warm_scales[:], rhs=warm_codes[:].bitcast(FP8X4), rhs_scale=warm_scales[:], start=True, stop=True)
-
         plane_first = sb.tile([P, RA_PASSES, K_PASS // 4], I32, name="plane_first")
         plane_second = sb.tile([P, RA_PASSES, K_PASS // 4], I32, name="plane_second")
         plane_rest = sb.tile([P, RA_PASSES, (L - 2 * K_PASS) // 4], I32, name="plane_rest")
@@ -272,7 +264,7 @@ def tile_clipped_overlap_covariance_s11_kernel(tc, ra, ovl_words, ovl_scales, wt
             nc.scalar.copy(out=consts[:], in_=bank[:].rearrange("p (t c) -> p t c", t=PACK)[:, :, 0:live])
 
         tick_words, diff_rows, ovl_rows = {}, {}, {}
-        for item in "Y00 Y01 d00 r0 c d01 r1 s0 o0 r2 r3 d10 d11 s1 o1 d20 d21 s2 o2 d30 d31 o3".split():
+        for item in "Y00 Y01 c d00 d01 R00 R01 d10 R10 R11 s0 o0 d11 s1 o1 d20 d21 s2 o2 d30 d31 o3".split():
             n = [int(c) for c in item if c in "0123456789"]
             if item[0] in "yr":
                 rows = load_ticks(yb if item[0] == "y" else ra, n[0], item[0])
@@ -303,12 +295,12 @@ def tile_clipped_overlap_covariance_s11_kernel(tc, ra, ovl_words, ovl_scales, wt
             else:
                 load_ovl_scales(plane_rest, K_PASS // 2, (L - 2 * K_PASS) // 4)
 
-        on_scalar = "Id011 Iv00 Iv01 Id111 Id20 Iv1 Id30 Iv2 Iu2 Iv31 Iu330 E0 E2".split()
+        on_scalar = "Tr00 Tr10 Id01 Id10 Id111 Iv00 Iv01 Id20 Iv1 Id30 Iu0 Iu1 Iu2 Iv31 E0 E1 E2 E3 M00 M12".split()
         yb_mx, ra_mx, u_mx, v_mx, diff_mx, ovl_mx, packs, held, slots = {}, {}, {}, {}, {}, {}, {}, {}, {}
         last = GROUPS - 1
         banks, sorted_scales = {}, {}
-        for item in """W18 use4567 Ty00 Ty10 Ty01 Ty11 W8 Id00 Qy0 Tr00 Tr01 Qd00 Qy1 Sk Vp000 Id010 Id011 Tc Qr0 Qd01 Tr10 Tr11 Vp01 Ss0 Sc0 C00 C01 Qr1 C02 C03
- Tr20 Tr21 Up000 Iv00 Qr2 Id10 Tr30 Tr31 Up01 Up02 Id110 Id111 Qr3 Qd10 Up03 Qd11 Iv01 Ss1 Sc1 M00 M01 use45670123 M02 M03 Vs10 C10 Vs11 C11 Vs12 C12 Vs13 C13 Id20 Id21 Qv0 Qd20 Us10 M10 Us11 M11 Qd21 Ss2 Sc2 Iv1 Iu0 Us12 Us13 Qu0 M12 M13 Vs20 C20 Vs21 C21 Vs22 C22 Vs23 C23 Id30 Id31 Qv1 Qd30 Us20 M20 Us21 M21 Qd31 Ss3 Sc3 Iv2 Iu1 Us22 Us23 Qu1 M22 M23 Vs30 C30 Vs31 C31 Vs32 C32 Vs33 C33 Iu2 Qv2 Us30 M30 Us31 M31 Iv30 Iv31 Us32 M32 Us33 M33 Qu2 Qv3 O00 O10 O20 O30 O01 O11 O21 O31 O02 O12 O22 O32 Iu300 Iu310 Qu30 Iu330 Iu320 Qu31 Qu32 Qu33 O03 E0 O13 E1 O23 E2 O33 E3""".split():
+        for item in """use01234567 Ty00 Ty10 Ty01 Ty11 Sk Tc Id00 Qy0 Qy1 Id01 Qd00 Tr00 Tr10 Qd01 Tr01 Tr11 Vs00 Qr0 C00 Vs01 C01 Vs02 C02 Id10 use5670 Tr20 Tr30 Vs03 Qr1 Qd10 Ss0 C03 Tr21 Tr31
+ Vp101 Sc0 Qr2 Qr3 Iv00 Id110 Id111 Ss1 Us00 M00 Qd11 Iv01 Us01 Sc1 M01 Us02 M02 Vp11 C10 C11 C12 C13 Id20 Us03 M03 Id21 Us10 M10 Us11 M11 Qd20 Qd21 Ss2 Sc2 Qv0 Id30 Us12 M12 Us13 M13 Vs20 C20 Vs21 C21 Vs22 C22 Vs23 C23 Iv1 Id31 Us20 M20 Us21 M21 Qd30 Qd31 Ss3 Sc3 Iu0 Qv1 Us22 M22 Us23 M23 Vs30 C30 Vs31 C31 Vs32 C32 Vs33 C33 Iu1 Qu0 Iv2 Ua0 Ua1 X0 Qu1 Iu2 Iv30 Qv2 X1 Iv31 Ob01 Ob12 Ob23 Ob34 Ua2 O01 O11 O21 O31 Ua3 Qu30 Qu2 Qu31 X2 Qv3 X3 Qu32 Qu33 O02 O03 E0 O12 O13 E1 O22 O23 E2 O32 O33 E3""".split():
             engine = "scalar" if item in on_scalar else "vector"
             n = [int(c) for c in item if c in "0123456789"]
             kind = "".join([c for c in item if c not in "0123456789"])
@@ -357,8 +349,6 @@ def tile_clipped_overlap_covariance_s11_kernel(tc, ra, ovl_words, ovl_scales, wt
                 sorted_scales[n[0]] = sort_scales(n[0], planes[n[0]])
             elif kind == "Sk":
                 sort_consts()
-            elif kind == "W":
-                warm(int(item[1:]))
             elif kind == "Vp" or kind == "Up":
                 name = ("v" if kind == "Vp" else "u") + str(n[0])
                 if n[1] == 0:
@@ -370,7 +360,7 @@ def tile_clipped_overlap_covariance_s11_kernel(tc, ra, ovl_words, ovl_scales, wt
                         u_pass(held[name][t], ovl_mx[n[0]], t, n[1], ra_mx[n[1]])
             elif kind == "Vs" or kind == "Us":
                 name = ("v" if kind == "Vs" else "u") + str(n[0])
-                bank = new_bank()
+                bank = new_bank(1 + n[1] if kind == "Vs" else (5 + n[1]) % 8)
                 held.setdefault(name, []).append(bank)
                 if kind == "Vs":
                     for g in range(YB_PASSES):
@@ -385,7 +375,33 @@ def tile_clipped_overlap_covariance_s11_kernel(tc, ra, ovl_words, ovl_scales, wt
                 if kind == "C":
                     clip(held[name][n[1]], slots[name], n[0], n[1])
                 else:
-                    weigh(held[name][n[1]], slots[name], n[0], n[1])
+                    weigh(held[name][n[1]], slots[name], n[0], n[1], "vector" if item in on_scalar else "scalar")
+            elif kind == "Ua":
+                bank = new_bank((5 + n[0]) % 8)
+                held["a%d" % n[0]] = bank
+                for t in range(PACK):
+                    for g in range(RA_PASSES):
+                        nc.tensor.matmul_mx(
+                            out=bank[:, t * P : (t + 1) * P],
+                            lhsT=ovl_mx[last][0][:, g, t * P // 2 : (t + 1) * P // 2].bitcast(FP4X4),
+                            lhsT_scale=ovl_mx[last][1][:, g, t * P // 4 : (t + 1) * P // 4].bitcast(U8),
+                            rhs=ra_mx[g][0][:, n[0] * P : (n[0] + 1) * P].bitcast(FP8X4),
+                            rhs_scale=ra_mx[g][1][:, n[0] * P : (n[0] + 1) * P],
+                            start=(g == 0),
+                            stop=(g == RA_PASSES - 1),
+                        )
+            elif kind == "X":
+                if "u3" not in packs:
+                    packs["u3"] = new_packed()
+                nc.vector.tensor_tensor(
+                    out=packs["u3"][:, n[0] * K_PASS : (n[0] + 1) * K_PASS].rearrange("p (i t) -> p i t", t=PACK),
+                    in0=held["a%d" % n[0]][:].rearrange("p (t i) -> p i t", t=PACK),
+                    in1=consts[:, :, last].unsqueeze(1).to_broadcast([P, P, PACK]),
+                    op=ALU.mult,
+                )
+            elif kind == "Ob":
+                banks[n[0]] = new_bank(n[1])
+                out_pass(banks[n[0]], n[0], 0)
             elif kind == "use":
                 turn[0], turn[1] = 0, n
             elif kind == "Vg" or kind == "Ug":

@@ -295,7 +295,7 @@ def tile_clipped_overlap_covariance_s11_kernel(tc, ra, ovl_words, ovl_scales, wt
             else:
                 load_ovl_scales(plane_rest, K_PASS // 2, (L - 2 * K_PASS) // 4)
 
-        on_scalar = "Tr00 Tr10 Id01 Id10 Id111 Iv00 Iv01 Id20 Iv1 Id30 Iu0 Iu1 Iu2 Iv31 E0 E1 E2 E3 M00 M12".split()
+        on_scalar = "Tr00 Tr10 Id01 Id10 Id111 Iv00 Iv01 Id20 Iv1 Id30 Iu0 Iu1 Iu2 Iv31 E0 E1 E2 E3 Iv30".split()
         yb_mx, ra_mx, u_mx, v_mx, diff_mx, ovl_mx, packs, held, slots = {}, {}, {}, {}, {}, {}, {}, {}, {}
         last = GROUPS - 1
         banks, sorted_scales = {}, {}

@@ -3,8 +3,8 @@ from contextlib import ExitStack
 import concourse.mybir as mybir
 from concourse.masks import make_identity
 
-ASSETS, TA, TB, L = 512, 2048, 1024, 2048
-FLOPS = 2 * ASSETS * (TA * L + TB * L + L * ASSETS)
+ASSETS, TICKS_A, TICKS_B, INTERVALS = 512, 2048, 1024, 2048
+FLOPS = 2 * ASSETS * (TICKS_A * INTERVALS + TICKS_B * INTERVALS + INTERVALS * ASSETS)
 
 F32 = mybir.dt.float32
 BF16 = mybir.dt.bfloat16
@@ -12,212 +12,202 @@ I32 = mybir.dt.int32
 U8 = mybir.dt.uint8
 FP8X4 = mybir.dt.float8_e4m3fn_x4
 FP4X4 = mybir.dt.float4_e2m1fn_x4
-ALU = mybir.AluOpType
-ACT = mybir.ActivationFunctionType
 
 P = 128
-PACK = 4
-K_PASS = P * PACK
-RA_PASSES, YB_PASSES, GROUPS = TA // K_PASS, TB // K_PASS, L // K_PASS
-TILES = ASSETS // P
+SLOTS = 4
+K_PASS = P * SLOTS
+RUN = 8
+RA_PASSES, YB_PASSES, GROUPS = TICKS_A // K_PASS, TICKS_B // K_PASS, INTERVALS // K_PASS
+ASSET_TILES = ASSETS // P
+CODE_WORDS = K_PASS // 2
+SCALE_WORDS = K_PASS // 4
+PACKED_BUFS = 8
 
 
 def tile_clipped_overlap_covariance_s11_kernel(tc, ra, ovl_words, ovl_scales, wt, yb, diff, lo, hi, out):
     nc = tc.nc
+    on_vector, on_scalar = nc.vector.tensor_copy, nc.scalar.copy
+
     with ExitStack() as ctx:
         sb = ctx.enter_context(tc.tile_pool(name="sb", bufs=1))
         psum = ctx.enter_context(tc.psum_pool(name="psum", bufs=1))
         ctx.enter_context(tc.manual_schedule())
 
-        def copy_on(engine, dst, src):
-            if engine == "scalar":
-                nc.scalar.copy(out=dst, in_=src)
-            else:
-                nc.vector.tensor_copy(out=dst, in_=src)
+        def u_bank(n):
+            return psum.tile([P, K_PASS], F32, name="u_bank%d" % n)
 
-        turn = [0, list(range(8))]
-
-        def new_bank(n=None):
-            if n is None:
-                n = turn[1][turn[0] % len(turn[1])]
-                turn[0] = turn[0] + 1
-            return psum.tile([P, K_PASS], F32, name="bank%d" % n)
+        def v_bank(n):
+            return psum.tile([P, K_PASS], F32, name="v_bank%d" % n)
 
         def new_packed():
-            return sb.tile([P, K_PASS * PACK], BF16, name="packed", bufs=8, align_bytes=64)
+            return sb.tile([P, K_PASS * SLOTS], BF16, name="packed", bufs=PACKED_BUFS, align_bytes=64)
 
-        def quantise(packed, name, c0=0, c1=K_PASS, into=None):
-            if into is None:
-                codes = sb.tile([P, K_PASS], I32, name=name + "_codes", align_bytes=64)
-                scales = sb.tile([P, K_PASS], U8, name=name + "_scales", align_bytes=64)
-                into = (codes, scales)
-            nc.vector.quantize_mx(out=into[0][:, c0:c1].bitcast(FP8X4), scales=into[1][:, c0:c1], in_=packed[:, PACK * c0 : PACK * c1])
-            return into
-
-        def load_ticks(src, g, name):
-            rows = sb.tile([P, TILES, K_PASS], BF16, name="%s_rows%d" % (name, g))
-            nc.sync.dma_start(out=rows[:], in_=src[:, g * K_PASS : (g + 1) * K_PASS].rearrange("(a p) k -> p a k", p=P))
-            return rows
-
-        def turn_ticks(rows, engines=("scalar", "scalar")):
-            packed = new_packed()
-            words = rows[:].bitcast(F32)
-            for half in range(2):
-                bank = new_bank()
-                for a in range(2):
-                    for u in range(2):
-                        c = (2 * a + u) * P
-                        nc.tensor.transpose(bank[:, c : c + P], words[:, 2 * half + a, u : 2 * P : 2], ident[:])
-                copy_on(
-                    engines[half],
-                    packed[:].bitcast(F32)[:, half * K_PASS : (half + 1) * K_PASS].rearrange("p (a i u) -> p a i u", a=2, u=2),
-                    bank[:].rearrange("p (a u i) -> p a i u", a=2, u=2),
-                )
-            return packed
-
-        def turn_half(words, packed, half, engine):
-            bank = new_bank()
-            for a in range(2):
-                for u in range(2):
-                    c = (2 * a + u) * P
-                    nc.tensor.transpose(bank[:, c : c + P], words[:, a, u : 2 * P : 2], ident[:])
-            copy_on(
-                engine,
-                packed[:].bitcast(F32)[:, half * K_PASS : (half + 1) * K_PASS].rearrange("p (a i u) -> p a i u", a=2, u=2),
-                bank[:].rearrange("p (a u i) -> p a i u", a=2, u=2),
-            )
-
-        def pack_diff_part(rows, packed, t0, t1, engine):
-            copy_on(
-                engine,
-                packed[:].rearrange("p (t q r j) -> p q t j r", t=PACK, r=8, j=PACK)[:, :, t0:t1],
-                rows.rearrange("p j (q t r) -> p q t j r", t=PACK, r=8)[:, :, t0:t1],
-            )
-
-        def load_diff(grp, g):
-            rows = sb.tile([P, PACK, K_PASS], BF16, name="diff_rows%d_%d" % (grp, g))
-            src = diff[g * K_PASS : (g + 1) * K_PASS, grp * K_PASS : (grp + 1) * K_PASS]
-            nc.sync.dma_start(out=rows[:], in_=src.rearrange("(p j) l -> p j l", j=PACK))
-            return rows
-
-        def pack_diff(rows, engine):
-            packed = new_packed()
-            copy_on(
-                engine,
-                packed[:].rearrange("p (t q r j) -> p q t j r", t=PACK, r=8, j=PACK),
-                rows[:].rearrange("p j (q t r) -> p q t j r", t=PACK, r=8),
-            )
-            return packed
-
-        def load_ovl(grp):
-            words = sb.tile([P, RA_PASSES, K_PASS // 2], I32, name="ovl_rows%d" % grp)
-            src = ovl_words.bitcast(I32)[:, :, grp * K_PASS // 2 : (grp + 1) * K_PASS // 2]
-            nc.sync.dma_start(out=words[:], in_=src.rearrange("g p w -> p g w"))
-            return words
-
-        def load_ovl_scales(plane, first_word, words):
-            src = ovl_scales.bitcast(I32)[:, :, first_word : first_word + words]
-            for r in range(4):
-                nc.sync.dma_start(out=plane[r:P:32, :, :], in_=src[:, r:16:4, :].rearrange("g q w -> q g w"))
-
-        def sort_ovl(grp, words, plane):
-            codes = sb.tile([P, RA_PASSES, K_PASS // 2], I32, name="ovl_codes%d" % grp, align_bytes=64)
-            scales = sb.tile([P, RA_PASSES, K_PASS // 4], I32, name="ovl_scales%d" % grp, align_bytes=64)
-            nc.vector.tensor_copy(
-                out=codes[:].rearrange("p g (t q w) -> p g t q w", t=PACK, w=4),
-                in_=words[:].rearrange("p g (q t w) -> p g t q w", t=PACK, w=4),
-            )
-            nc.vector.tensor_copy(
-                out=scales[:].rearrange("p g (t q w) -> p g t q w", t=PACK, w=2),
-                in_=plane.rearrange("p g (q t w) -> p g t q w", t=PACK, w=2),
-            )
+        def new_mx(name):
+            codes = sb.tile([P, K_PASS], I32, name=name + "_codes", align_bytes=64)
+            scales = sb.tile([P, K_PASS], U8, name=name + "_scales", align_bytes=64)
             return codes, scales
 
-        def sort_codes(grp, words):
-            codes = sb.tile([P, RA_PASSES, K_PASS // 2], I32, name="ovl_codes%d" % grp, align_bytes=64)
+        def quantise_columns(mx, packed, first, stop):
+            nc.vector.quantize_mx(
+                out=mx[0][:, first:stop].bitcast(FP8X4),
+                scales=mx[1][:, first:stop],
+                in_=packed[:, SLOTS * first : SLOTS * stop],
+            )
+
+        def quantise(packed, name):
+            mx = new_mx(name)
+            quantise_columns(mx, packed, 0, K_PASS)
+            return mx
+
+        tick_words, tick_packed = {}, {}
+
+        def load_ticks(name, src, first_pass, half):
+            rows = sb.tile([P, 2, 2 * K_PASS], BF16, name="%s_rows%d_%d" % (name, first_pass, half))
+            part = src[half * 2 * P : (half + 1) * 2 * P, first_pass * K_PASS : (first_pass + 2) * K_PASS]
+            nc.sync.dma_start(out=rows[:], in_=part.rearrange("(a p) k -> p a k", p=P))
+            for g in range(2):
+                tick_words[name, first_pass + g, half] = rows[:].bitcast(F32)[:, :, g * 2 * P : (g + 1) * 2 * P]
+
+        def turn_ticks(name, g, half, copy):
+            if half == 0:
+                tick_packed[name, g] = new_packed()
+            bank = u_bank(2 * half + g % 2)
+            for a in range(2):
+                for u in range(2):
+                    column = (2 * a + u) * P
+                    nc.tensor.transpose(bank[:, column : column + P], tick_words[name, g, half][:, a, u : 2 * P : 2], ident[:])
+            words = tick_packed[name, g][:].bitcast(F32)[:, half * K_PASS : (half + 1) * K_PASS]
+            copy(out=words.rearrange("p (a i u) -> p a i u", a=2, u=2), in_=bank[:].rearrange("p (a u i) -> p a i u", a=2, u=2))
+
+        diff_rows, diff_packed, diff_mx = {}, {}, {}
+
+        def load_diff(grp, g):
+            rows = sb.tile([P, SLOTS, K_PASS], BF16, name="diff_rows%d_%d" % (grp, g))
+            part = diff[g * K_PASS : (g + 1) * K_PASS, grp * K_PASS : (grp + 1) * K_PASS]
+            nc.sync.dma_start(out=rows[:], in_=part.rearrange("(p j) l -> p j l", j=SLOTS))
+            diff_rows[grp, g] = rows
+
+        def pack_diff(grp, g, copy, first=0, stop=SLOTS):
+            if first == 0:
+                diff_packed[grp, g] = new_packed()
+            copy(
+                out=diff_packed[grp, g][:].rearrange("p (t q r j) -> p q t j r", t=SLOTS, r=RUN, j=SLOTS)[:, :, first:stop],
+                in_=diff_rows[grp, g][:].rearrange("p j (q t r) -> p q t j r", t=SLOTS, r=RUN)[:, :, first:stop],
+            )
+
+        def quantise_diff(grp, g):
+            diff_mx[grp, g] = quantise(diff_packed[grp, g], "diff%d_%d" % (grp, g))
+
+        ovl_rows, ovl_codes, ovl_planes = {}, {}, {}
+
+        def load_ovl(grp):
+            words = sb.tile([P, RA_PASSES, CODE_WORDS], I32, name="ovl_rows%d" % grp)
+            part = ovl_words.bitcast(I32)[:, :, grp * CODE_WORDS : (grp + 1) * CODE_WORDS]
+            nc.sync.dma_start(out=words[:], in_=part.rearrange("g p w -> p g w"))
+            ovl_rows[grp] = words
+
+        def load_ovl_scales(rows, first_grp, stop_grp):
+            part = ovl_scales.bitcast(I32)[:, :, first_grp * SCALE_WORDS : stop_grp * SCALE_WORDS]
+            for r in range(4):
+                nc.sync.dma_start(out=rows[r:P:32, :, :], in_=part[:, r:16:4, :].rearrange("g q w -> q g w"))
+
+        def sort_by_slot(src, words, name):
+            dst = sb.tile([P, RA_PASSES, words], I32, name=name, align_bytes=64)
+            run = words * RUN // K_PASS
             nc.vector.tensor_copy(
-                out=codes[:].rearrange("p g (t q w) -> p g t q w", t=PACK, w=4),
-                in_=words[:].rearrange("p g (q t w) -> p g t q w", t=PACK, w=4),
+                out=dst[:].rearrange("p g (t q w) -> p g t q w", t=SLOTS, w=run),
+                in_=src.rearrange("p g (q t w) -> p g t q w", t=SLOTS, w=run),
             )
-            return codes
+            return dst
 
-        def sort_scales(grp, plane):
-            scales = sb.tile([P, RA_PASSES, K_PASS // 4], I32, name="ovl_scales%d" % grp, align_bytes=64)
-            nc.vector.tensor_copy(
-                out=scales[:].rearrange("p g (t q w) -> p g t q w", t=PACK, w=2),
-                in_=plane.rearrange("p g (q t w) -> p g t q w", t=PACK, w=2),
-            )
-            return scales
+        def sort_ovl_scales(grp):
+            ovl_planes[grp] = sort_by_slot(scale_rows[grp], SCALE_WORDS, "ovl_plane%d" % grp)
 
-        def u_pass(bank, ovl_mx, t, g, ra_g):
+        def sort_ovl_codes(grp):
+            ovl_codes[grp] = sort_by_slot(ovl_rows[grp][:], CODE_WORDS, "ovl_codes%d" % grp)
+
+        ra_mx, yb_mx, u_mx, v_mx = {}, {}, {}, {}
+        u_sums, v_sums, u_slots, v_slots, u_packed, v_packed = {}, {}, {}, {}, {}, {}
+
+        def u_slot(grp, t):
+            u_sums[t] = u_bank(t)
+            for g in range(RA_PASSES):
+                nc.tensor.matmul_mx(
+                    out=u_sums[t][:],
+                    lhsT=ovl_codes[grp][:, g, t * CODE_WORDS // SLOTS : (t + 1) * CODE_WORDS // SLOTS].bitcast(FP4X4),
+                    lhsT_scale=ovl_planes[grp][:, g, t * SCALE_WORDS // SLOTS : (t + 1) * SCALE_WORDS // SLOTS].bitcast(U8),
+                    rhs=ra_mx[g][0][:].bitcast(FP8X4),
+                    rhs_scale=ra_mx[g][1][:],
+                    start=(g == 0),
+                    stop=(g == RA_PASSES - 1),
+                )
+
+        def v_pass(grp, t, g):
+            if g == 0:
+                v_sums[t] = v_bank(t)
             nc.tensor.matmul_mx(
-                out=bank[:],
-                lhsT=ovl_mx[0][:, g, t * P // 2 : (t + 1) * P // 2].bitcast(FP4X4),
-                lhsT_scale=ovl_mx[1][:, g, t * P // 4 : (t + 1) * P // 4].bitcast(U8),
-                rhs=ra_g[0][:].bitcast(FP8X4),
-                rhs_scale=ra_g[1][:],
-                start=(g == 0),
-                stop=(g == RA_PASSES - 1),
-            )
-
-        def v_pass(bank, diff_g, t, g, yb_g):
-            nc.tensor.matmul_mx(
-                out=bank[:],
-                lhsT=diff_g[0][:, t * P : (t + 1) * P].bitcast(FP8X4),
-                lhsT_scale=diff_g[1][:, t * P : (t + 1) * P],
-                rhs=yb_g[0][:].bitcast(FP8X4),
-                rhs_scale=yb_g[1][:],
+                out=v_sums[t][:],
+                lhsT=diff_mx[grp, g][0][:, t * P : (t + 1) * P].bitcast(FP8X4),
+                lhsT_scale=diff_mx[grp, g][1][:, t * P : (t + 1) * P],
+                rhs=yb_mx[g][0][:].bitcast(FP8X4),
+                rhs_scale=yb_mx[g][1][:],
                 start=(g == 0),
                 stop=(g == YB_PASSES - 1),
             )
 
-        def new_slots():
-            return sb.tile([P, PACK, ASSETS], BF16, name="slots", bufs=8)
+        def v_slot(grp, t):
+            for g in range(YB_PASSES):
+                v_pass(grp, t, g)
 
-        def weigh(bank, slots, grp, t, engine="scalar"):
-            if engine == "scalar":
-                nc.scalar.activation(out=slots[:, t, :], in_=bank[:], func=ACT.Copy, scale=consts[:, t, grp : grp + 1])
-            else:
-                nc.vector.tensor_scalar_mul(out=slots[:, t, :], in0=bank[:], scalar1=consts[:, t, grp : grp + 1])
+        def weigh(grp, t):
+            if t == 0:
+                u_slots[grp] = sb.tile([P, SLOTS, ASSETS], BF16, name="u_slots%d" % grp)
+            nc.scalar.activation(
+                out=u_slots[grp][:, t, :],
+                in_=u_sums[t][:],
+                func=mybir.ActivationFunctionType.Copy,
+                scale=per_interval[:, t, grp : grp + 1],
+            )
 
-        def clip(bank, slots, grp, t):
+        def clip(grp, t):
+            if t == 0:
+                v_slots[grp] = sb.tile([P, SLOTS, ASSETS], BF16, name="v_slots%d" % grp)
             nc.vector.tensor_scalar(
-                out=slots[:, t, :],
-                in0=bank[:],
-                scalar1=consts[:, t, GROUPS + grp : GROUPS + grp + 1],
-                scalar2=consts[:, t, 2 * GROUPS + grp : 2 * GROUPS + grp + 1],
-                op0=ALU.max,
-                op1=ALU.min,
+                out=v_slots[grp][:, t, :],
+                in0=v_sums[t][:],
+                scalar1=per_interval[:, t, GROUPS + grp : GROUPS + grp + 1],
+                scalar2=per_interval[:, t, 2 * GROUPS + grp : 2 * GROUPS + grp + 1],
+                op0=mybir.AluOpType.max,
+                op1=mybir.AluOpType.min,
             )
 
-        def pack_slots(slots, engine, packed=None, c0=0, c1=ASSETS):
-            if packed is None:
-                packed = new_packed()
-            copy_on(
-                engine,
-                packed[:, PACK * c0 : PACK * c1].rearrange("p (c i t) -> p c t i", i=4, t=PACK),
-                slots[:, :, c0:c1].rearrange("p t (c i) -> p c t i", i=4),
+        def pack_slots(slots, packed, grp, copy, first=0, stop=ASSETS):
+            if first == 0:
+                packed[grp] = new_packed()
+            copy(
+                out=packed[grp][:, SLOTS * first : SLOTS * stop].rearrange("p (c i t) -> p c t i", i=4, t=SLOTS),
+                in_=slots[grp][:, :, first:stop].rearrange("p t (c i) -> p c t i", i=4),
             )
-            return packed
 
-        def v_group(grp, diff_mx):
-            slots = new_slots()
-            for t in range(PACK):
-                bank = new_bank()
-                for g in range(YB_PASSES):
-                    v_pass(bank, diff_mx[g], t, g, yb_mx[g])
-                clip(bank, slots, grp, t)
-            return slots
+        def pack_u(grp, copy, first=0, stop=ASSETS):
+            pack_slots(u_slots, u_packed, grp, copy, first, stop)
 
-        def u_slot(grp, ovl_mx, slots, t):
-            bank = new_bank()
-            for g in range(RA_PASSES):
-                u_pass(bank, ovl_mx, t, g, ra_mx[g])
-            weigh(bank, slots, grp, t)
+        def pack_v(grp, copy, first=0, stop=ASSETS):
+            pack_slots(v_slots, v_packed, grp, copy, first, stop)
 
-        def out_pass(bank, a, grp):
+        def quantise_u(grp):
+            u_mx[grp] = quantise(u_packed[grp], "u%d" % grp)
+
+        def quantise_v(grp):
+            v_mx[grp] = quantise(v_packed[grp], "v%d" % grp)
+
+        out_sums = {}
+
+        def out_pass(a, grp):
+            if grp == 0:
+                out_sums[a] = v_bank(a)
             nc.tensor.matmul_mx(
-                out=bank[:],
+                out=out_sums[a][:],
                 lhsT=u_mx[grp][0][:, a * P : (a + 1) * P].bitcast(FP8X4),
                 lhsT_scale=u_mx[grp][1][:, a * P : (a + 1) * P],
                 rhs=v_mx[grp][0][:].bitcast(FP8X4),
@@ -226,207 +216,153 @@ def tile_clipped_overlap_covariance_s11_kernel(tc, ra, ovl_words, ovl_scales, wt
                 stop=(grp == GROUPS - 1),
             )
 
-        def store(bank, a, engine):
-            res = sb.tile([P, ASSETS], F32, name="res%d" % a)
-            copy_on(engine, res[:], bank[:])
-            nc.sync.dma_start(out=out[a * P : (a + 1) * P, :], in_=res[:])
+        def store(a):
+            result = sb.tile([P, ASSETS], F32, name="result%d" % a)
+            nc.scalar.copy(out=result[:], in_=out_sums[a][:])
+            nc.sync.dma_start(out=out[a * P : (a + 1) * P, :], in_=result[:])
 
         ident = sb.tile([P, P], F32, name="ident")
         make_identity(nc, ident[:])
-        const_sorted = sb.tile([P, K_PASS], F32, name="const_sorted")
-        nc.gpsimd.memset(const_sorted[:], 0.0)
-        plane_first = sb.tile([P, RA_PASSES, K_PASS // 4], I32, name="plane_first")
-        plane_second = sb.tile([P, RA_PASSES, K_PASS // 4], I32, name="plane_second")
-        plane_rest = sb.tile([P, RA_PASSES, (L - 2 * K_PASS) // 4], I32, name="plane_rest")
-        nc.vector.memset(plane_first[:], 0)
-        nc.vector.memset(plane_second[:], 0)
-        nc.vector.memset(plane_rest[:], 0)
-        planes = [plane_first[:], plane_second[:]] + [plane_rest[:, :, i * K_PASS // 4 : (i + 1) * K_PASS // 4] for i in range(GROUPS - 2)]
-        const_rows = sb.tile([P, K_PASS], BF16, name="const_rows")
-        consts = sb.tile([P, PACK, 3 * GROUPS], F32, name="consts")
+        vector_count = 3 * GROUPS
+        vector_rows = sb.tile([P, K_PASS], BF16, name="vector_rows")
+        vector_sorted = sb.tile([P, K_PASS], F32, name="vector_sorted")
+        per_interval = sb.tile([P, SLOTS, vector_count], F32, name="per_interval")
+        nc.gpsimd.memset(vector_sorted[:], 0.0)
+        scale_tiles = [sb.tile([P, RA_PASSES, n * SCALE_WORDS], I32, name="scale_rows%d" % i) for i, n in enumerate((1, 1, 2))]
+        for zeroed in scale_tiles:
+            nc.vector.memset(zeroed[:], 0)
+        scale_rows = [scale_tiles[0][:], scale_tiles[1][:], scale_tiles[2][:, :, 0:SCALE_WORDS], scale_tiles[2][:, :, SCALE_WORDS:]]
 
-        def load_consts():
-            for n, vec in enumerate((wt, lo, hi)):
-                nc.sync.dma_start(out=const_rows[n * GROUPS : (n + 1) * GROUPS, :], in_=vec.rearrange("(g l) -> g l", g=GROUPS))
+        for half in range(2):
+            load_ticks("yb", yb, 0, half)
+        for n, vec in enumerate((wt, lo, hi)):
+            nc.sync.dma_start(out=vector_rows[n * GROUPS : (n + 1) * GROUPS, :], in_=vec.rearrange("(g l) -> g l", g=GROUPS))
+        load_diff(0, 0)
+        load_diff(0, 1)
+        for half in range(2):
+            load_ticks("ra", ra, 0, half)
+        load_diff(1, 0)
+        for half in range(2):
+            load_ticks("ra", ra, 2, half)
+        load_ovl_scales(scale_tiles[0], 0, 1)
+        load_ovl(0)
+        load_diff(1, 1)
+        load_diff(2, 0)
+        load_ovl_scales(scale_tiles[1], 1, 2)
+        load_ovl(1)
+        load_diff(2, 1)
+        load_diff(3, 0)
+        load_ovl_scales(scale_tiles[2], 2, GROUPS)
+        load_ovl(2)
+        load_diff(3, 1)
+        load_ovl(3)
 
-        live = 3 * GROUPS
+        for half in range(2):
+            for g in range(YB_PASSES):
+                turn_ticks("yb", g, half, on_scalar)
+        nc.vector.tensor_copy(
+            out=vector_sorted[0:vector_count, :].rearrange("p (t q r) -> p t q r", t=SLOTS, r=RUN),
+            in_=vector_rows[0:vector_count, :].rearrange("p (q t r) -> p t q r", t=SLOTS, r=RUN),
+        )
+        vector_bank = v_bank(SLOTS - 1)
+        for t in range(SLOTS):
+            nc.tensor.transpose(vector_bank[:, t * P : (t + 1) * P], vector_sorted[:, t * P : (t + 1) * P], ident[:])
+        nc.scalar.copy(out=per_interval[:], in_=vector_bank[:].rearrange("p (t c) -> p t c", t=SLOTS)[:, :, 0:vector_count])
+        pack_diff(0, 0, on_vector)
+        for g in range(YB_PASSES):
+            yb_mx[g] = quantise(tick_packed["yb", g], "yb%d" % g)
+        pack_diff(0, 1, on_scalar)
+        quantise_diff(0, 0)
 
-        def sort_consts():
-            nc.vector.tensor_copy(
-                out=const_sorted[0:live, :].rearrange("p (t q r) -> p t q r", t=PACK, r=8),
-                in_=const_rows[0:live, :].rearrange("p (q t r) -> p t q r", t=PACK, r=8),
-            )
+        for g in range(2):
+            turn_ticks("ra", g, 0, on_vector)
+        quantise_diff(0, 1)
+        for g in range(2):
+            turn_ticks("ra", g, 1, on_scalar)
+        ra_mx[0] = quantise(tick_packed["ra", 0], "ra0")
+        for t in range(SLOTS - 1):
+            v_slot(0, t)
+            clip(0, t)
+        pack_diff(1, 0, on_scalar)
+        for g in range(2, RA_PASSES):
+            turn_ticks("ra", g, 0, on_scalar)
+        v_slot(0, SLOTS - 1)
+        ra_mx[1] = quantise(tick_packed["ra", 1], "ra1")
+        quantise_diff(1, 0)
+        sort_ovl_scales(0)
+        clip(0, SLOTS - 1)
+        for g in range(2, RA_PASSES):
+            turn_ticks("ra", g, 1, on_scalar)
+        for t in range(SLOTS):
+            v_pass(1, t, 0)
+        sort_ovl_codes(0)
+        for g in range(2, RA_PASSES):
+            ra_mx[g] = quantise(tick_packed["ra", g], "ra%d" % g)
 
-        def turn_consts():
-            bank = new_bank()
-            for t in range(PACK):
-                nc.tensor.transpose(bank[:, t * P : (t + 1) * P], const_sorted[:, t * P : (t + 1) * P], ident[:])
-            nc.scalar.copy(out=consts[:], in_=bank[:].rearrange("p (t c) -> p t c", t=PACK)[:, :, 0:live])
+        pack_v(0, on_scalar, 0, ASSETS // 2)
+        pack_diff(1, 1, on_vector, 0, SLOTS // 2)
+        pack_diff(1, 1, on_scalar, SLOTS // 2, SLOTS)
+        pack_v(0, on_vector, ASSETS // 2, ASSETS)
+        quantise_diff(1, 1)
+        for t in range(2):
+            u_slot(0, t)
+            weigh(0, t)
+        pack_diff(2, 0, on_scalar)
+        sort_ovl_scales(1)
+        sort_ovl_codes(1)
+        u_slot(0, 2)
+        for t in range(SLOTS):
+            v_pass(1, t, 1)
+            clip(1, t)
+        u_slot(0, 3)
+        for t in range(2, SLOTS):
+            weigh(0, t)
 
-        tick_words, diff_rows, ovl_rows = {}, {}, {}
-        for item in "Y00 Y01 c d00 d01 R00 R01 d10 R10 R11 s0 o0 d11 s1 o1 d20 d21 s2 o2 d30 d31 o3".split():
-            n = [int(c) for c in item if c in "0123456789"]
-            if item[0] in "yr":
-                rows = load_ticks(yb if item[0] == "y" else ra, n[0], item[0])
-                for h in range(2):
-                    tick_words[item[0], n[0], h] = rows[:].bitcast(F32)[:, 2 * h : 2 * h + 2, :]
-            elif item[0] in "YR":
-                src = yb if item[0] == "Y" else ra
-                rows = sb.tile([P, 2, 2 * K_PASS], BF16, name=item)
-                nc.sync.dma_start(out=rows[:], in_=src[n[1] * 2 * P : (n[1] + 1) * 2 * P, n[0] * 2 * K_PASS : (n[0] + 1) * 2 * K_PASS].rearrange("(a p) k -> p a k", p=P))
-                for g in range(2):
-                    tick_words["y" if item[0] == "Y" else "r", 2 * n[0] + g, n[1]] = rows[:].bitcast(F32)[:, :, g * 2 * P : (g + 1) * 2 * P]
-            elif item[0] == "d":
-                diff_rows[n[0], n[1]] = load_diff(n[0], n[1])[:]
-            elif item[0] == "D":
-                rows = sb.tile([P, PACK, 2 * K_PASS], BF16, name=item)
-                src = diff[n[1] * K_PASS : (n[1] + 1) * K_PASS, n[0] * 2 * K_PASS : (n[0] + 1) * 2 * K_PASS]
-                nc.sync.dma_start(out=rows[:], in_=src.rearrange("(p j) l -> p j l", j=PACK))
-                for i in range(2):
-                    diff_rows[2 * n[0] + i, n[1]] = rows[:, :, i * K_PASS : (i + 1) * K_PASS]
-            elif item[0] == "o":
-                ovl_rows[n[0]] = load_ovl(n[0])
-            elif item == "c":
-                load_consts()
-            elif item == "s0":
-                load_ovl_scales(plane_first, 0, K_PASS // 4)
-            elif item == "s1":
-                load_ovl_scales(plane_second, K_PASS // 4, K_PASS // 4)
-            else:
-                load_ovl_scales(plane_rest, K_PASS // 2, (L - 2 * K_PASS) // 4)
-
-        on_scalar = "Tr00 Tr10 Id01 Id10 Id111 Iv00 Iv01 Id20 Iv1 Id30 Iu0 Iu1 Iu2 Iv31 E0 E1 E2 E3 Iv30".split()
-        yb_mx, ra_mx, u_mx, v_mx, diff_mx, ovl_mx, packs, held, slots = {}, {}, {}, {}, {}, {}, {}, {}, {}
         last = GROUPS - 1
-        banks, sorted_scales = {}, {}
-        for item in """use01234567 Ty00 Ty10 Ty01 Ty11 Sk Tc Id00 Qy0 Qy1 Id01 Qd00 Tr00 Tr10 Qd01 Tr01 Tr11 Vs00 Qr0 C00 Vs01 C01 Vs02 C02 Id10 use5670 Tr20 Tr30 Vs03 Qr1 Qd10 Ss0 C03 Tr21 Tr31
- Vp101 Sc0 Qr2 Qr3 Iv00 Id110 Id111 Ss1 Us00 M00 Qd11 Iv01 Us01 Sc1 M01 Us02 M02 Vp11 C10 C11 C12 C13 Id20 Us03 M03 Id21 Us10 M10 Us11 M11 Qd20 Qd21 Ss2 Sc2 Qv0 Id30 Us12 M12 Us13 M13 Vs20 C20 Vs21 C21 Vs22 C22 Vs23 C23 Iv1 Id31 Us20 M20 Us21 M21 Qd30 Qd31 Ss3 Sc3 Iu0 Qv1 Us22 M22 Us23 M23 Vs30 C30 Vs31 C31 Vs32 C32 Vs33 C33 Iu1 Qu0 Iv2 Ua0 Ua1 X0 Qu1 Iu2 Iv30 Qv2 X1 Iv31 Ob01 Ob12 Ob23 Ob34 Ua2 O01 O11 O21 O31 Ua3 Qu30 Qu2 Qu31 X2 Qv3 X3 Qu32 Qu33 O02 O03 E0 O12 O13 E1 O22 O23 E2 O32 O33 E3""".split():
-            engine = "scalar" if item in on_scalar else "vector"
-            n = [int(c) for c in item if c in "0123456789"]
-            kind = "".join([c for c in item if c not in "0123456789"])
-            if kind == "Ty" or kind == "Tr":
-                key = item[1:3]
-                if key not in packs:
-                    packs[key] = new_packed()
-                turn_half(tick_words[item[1], n[0], n[1]], packs[key], n[1], "vector" if item in on_scalar else "scalar")
-            elif kind == "Tc":
-                turn_consts()
-            elif kind == "Id":
-                key = item[1:4]
-                if key not in packs:
-                    packs[key] = new_packed()
-                if len(n) == 2:
-                    pack_diff_part(diff_rows[n[0], n[1]], packs[key], 0, 4, engine)
-                else:
-                    pack_diff_part(diff_rows[n[0], n[1]], packs[key], 2 * n[2], 2 * n[2] + 2, engine)
-            elif kind == "Iu" or kind == "Iv":
-                key = item[1:3]
-                if key not in packs:
-                    packs[key] = new_packed()
-                if len(n) == 1:
-                    pack_slots(slots[key], engine, packs[key])
-                elif len(n) == 2:
-                    pack_slots(slots[key], engine, packs[key], 2 * P * n[1], 2 * P * (n[1] + 1))
-                else:
-                    pack_slots(slots[key], engine, packs[key], P * n[1], P * (n[1] + 1))
-            elif kind == "Qy":
-                yb_mx[n[0]] = quantise(packs[item[1:]], item)
-            elif kind == "Qr":
-                ra_mx[n[0]] = quantise(packs[item[1:]], item)
-            elif kind == "Qd":
-                diff_mx[n[0], n[1]] = quantise(packs[item[1:]], item)
-            elif kind == "Qu" and len(n) == 1:
-                u_mx[n[0]] = quantise(packs[item[1:]], item)
-            elif kind == "Qu":
-                u_mx[n[0]] = quantise(packs[item[1:3]], item[0:3], n[1] * P, (n[1] + 1) * P, u_mx.get(n[0]))
-            elif kind == "Qv":
-                v_mx[n[0]] = quantise(packs[item[1:]], item)
-            elif kind == "S":
-                ovl_mx[n[0]] = sort_ovl(n[0], ovl_rows[n[0]], planes[n[0]])
-            elif kind == "Sc":
-                ovl_mx[n[0]] = (sort_codes(n[0], ovl_rows[n[0]]), sorted_scales[n[0]])
-            elif kind == "Ss":
-                sorted_scales[n[0]] = sort_scales(n[0], planes[n[0]])
-            elif kind == "Sk":
-                sort_consts()
-            elif kind == "Vp" or kind == "Up":
-                name = ("v" if kind == "Vp" else "u") + str(n[0])
-                if n[1] == 0:
-                    held[name] = [new_bank(n[2] + t) for t in range(PACK)]
-                for t in range(PACK):
-                    if kind == "Vp":
-                        v_pass(held[name][t], diff_mx[n[0], n[1]], t, n[1], yb_mx[n[1]])
-                    else:
-                        u_pass(held[name][t], ovl_mx[n[0]], t, n[1], ra_mx[n[1]])
-            elif kind == "Vs" or kind == "Us":
-                name = ("v" if kind == "Vs" else "u") + str(n[0])
-                bank = new_bank(1 + n[1] if kind == "Vs" else (5 + n[1]) % 8)
-                held.setdefault(name, []).append(bank)
-                if kind == "Vs":
-                    for g in range(YB_PASSES):
-                        v_pass(bank, diff_mx[n[0], g], n[1], g, yb_mx[g])
-                else:
-                    for g in range(RA_PASSES):
-                        u_pass(bank, ovl_mx[n[0]], n[1], g, ra_mx[g])
-            elif kind == "C" or kind == "M":
-                name = ("v" if kind == "C" else "u") + str(n[0])
-                if n[1] == 0:
-                    slots[name] = new_slots()
-                if kind == "C":
-                    clip(held[name][n[1]], slots[name], n[0], n[1])
-                else:
-                    weigh(held[name][n[1]], slots[name], n[0], n[1], "vector" if item in on_scalar else "scalar")
-            elif kind == "Ua":
-                bank = new_bank((5 + n[0]) % 8)
-                held["a%d" % n[0]] = bank
-                for t in range(PACK):
-                    for g in range(RA_PASSES):
-                        nc.tensor.matmul_mx(
-                            out=bank[:, t * P : (t + 1) * P],
-                            lhsT=ovl_mx[last][0][:, g, t * P // 2 : (t + 1) * P // 2].bitcast(FP4X4),
-                            lhsT_scale=ovl_mx[last][1][:, g, t * P // 4 : (t + 1) * P // 4].bitcast(U8),
-                            rhs=ra_mx[g][0][:, n[0] * P : (n[0] + 1) * P].bitcast(FP8X4),
-                            rhs_scale=ra_mx[g][1][:, n[0] * P : (n[0] + 1) * P],
-                            start=(g == 0),
-                            stop=(g == RA_PASSES - 1),
-                        )
-            elif kind == "X":
-                if "u3" not in packs:
-                    packs["u3"] = new_packed()
-                nc.vector.tensor_tensor(
-                    out=packs["u3"][:, n[0] * K_PASS : (n[0] + 1) * K_PASS].rearrange("p (i t) -> p i t", t=PACK),
-                    in0=held["a%d" % n[0]][:].rearrange("p (t i) -> p i t", t=PACK),
-                    in1=consts[:, :, last].unsqueeze(1).to_broadcast([P, P, PACK]),
-                    op=ALU.mult,
-                )
-            elif kind == "Ob":
-                banks[n[0]] = new_bank(n[1])
-                out_pass(banks[n[0]], n[0], 0)
-            elif kind == "use":
-                turn[0], turn[1] = 0, n
-            elif kind == "Vg" or kind == "Ug":
-                name = ("v" if kind == "Vg" else "u") + str(n[0])
-                if n[1] == 0:
-                    held[name] = [new_bank(n[2] + t) for t in range(PACK)]
-                    slots[name] = new_slots()
-                for t in range(PACK):
-                    if kind == "Vg":
-                        v_pass(held[name][t], diff_mx[n[0], n[1]], t, n[1], yb_mx[n[1]])
-                        if n[1] == YB_PASSES - 1:
-                            clip(held[name][t], slots[name], n[0], t)
-                    else:
-                        u_pass(held[name][t], ovl_mx[n[0]], t, n[1], ra_mx[n[1]])
-                        if n[1] == RA_PASSES - 1:
-                            weigh(held[name][t], slots[name], n[0], t)
-            elif kind == "V":
-                slots["v%d" % n[0]] = v_group(n[0], [diff_mx[n[0], 0], diff_mx[n[0], 1]])
-            elif kind == "Ut":
-                if n[1] == 0:
-                    slots["u%d" % n[0]] = new_slots()
-                u_slot(n[0], ovl_mx[n[0]], slots["u%d" % n[0]], n[1])
-            elif kind == "O":
-                if n[1] == 0:
-                    banks[n[0]] = new_bank()
-                out_pass(banks[n[0]], n[0], n[1])
-            elif kind == "E":
-                store(banks[n[0]], n[0], engine)
+        scalar_packs = {
+            1: [lambda: pack_diff(last, 0, on_scalar)],
+            2: [lambda: pack_v(1, on_scalar), lambda: pack_u(0, on_scalar)],
+            3: [lambda: pack_u(1, on_scalar), lambda: pack_u(2, on_scalar)],
+        }
+        for grp in range(1, GROUPS):
+            scalar_packs[grp][0]()
+            u_slot(grp, 0)
+            weigh(grp, 0)
+            for pack in scalar_packs[grp][1:]:
+                pack()
+            for t in range(1, SLOTS):
+                u_slot(grp, t)
+                weigh(grp, t)
+            if grp < last:
+                pack_diff(grp + 1, 1, on_vector)
+                for g in range(YB_PASSES):
+                    quantise_diff(grp + 1, g)
+                sort_ovl_scales(grp + 1)
+                sort_ovl_codes(grp + 1)
+                quantise_v(grp - 1)
+                for t in range(SLOTS):
+                    v_slot(grp + 1, t)
+                    clip(grp + 1, t)
+
+        quantise_u(0)
+        pack_v(2, on_vector)
+        quantise_u(1)
+        pack_v(last, on_vector)
+        quantise_v(2)
+        quantise_u(2)
+        quantise_v(last)
+        u_mx[last] = new_mx("u%d" % last)
+        for a in range(2):
+            pack_u(last, on_scalar, a * P, (a + 1) * P)
+        for a in range(ASSET_TILES):
+            quantise_columns(u_mx[last], u_packed[last], a * P, (a + 1) * P)
+            if a + 2 < ASSET_TILES:
+                pack_u(last, on_vector, (a + 2) * P, (a + 3) * P)
+
+        for grp in range(2):
+            for a in range(ASSET_TILES):
+                out_pass(a, grp)
+        for a in range(ASSET_TILES):
+            for grp in range(2, GROUPS):
+                out_pass(a, grp)
+            store(a)

@@ -129,18 +129,28 @@ def tile_clipped_overlap_covariance_s11_kernel(tc, ra, ovl_words, ovl_scales, wt
         ra_mx, yb_mx, u_mx, v_mx = {}, {}, {}, {}
         u_sums, v_sums, u_slots, v_slots, u_packed, v_packed = {}, {}, {}, {}, {}, {}
 
-        def u_slot(grp, t):
-            u_sums[t] = u_bank(t)
-            for g in range(RA_PASSES):
-                nc.tensor.matmul_mx(
-                    out=u_sums[t][:],
-                    lhsT=ovl_codes[grp][:, g, t * CODE_WORDS // SLOTS : (t + 1) * CODE_WORDS // SLOTS].bitcast(FP4X4),
-                    lhsT_scale=ovl_planes[grp][:, g, t * SCALE_WORDS // SLOTS : (t + 1) * SCALE_WORDS // SLOTS].bitcast(U8),
-                    rhs=ra_mx[g][0][:].bitcast(FP8X4),
-                    rhs_scale=ra_mx[g][1][:],
-                    start=(g == 0),
-                    stop=(g == RA_PASSES - 1),
-                )
+        def u_matmul(sums, grp, t, g, assets):
+            nc.tensor.matmul_mx(
+                out=sums,
+                lhsT=ovl_codes[grp][:, g, t * CODE_WORDS // SLOTS : (t + 1) * CODE_WORDS // SLOTS].bitcast(FP4X4),
+                lhsT_scale=ovl_planes[grp][:, g, t * SCALE_WORDS // SLOTS : (t + 1) * SCALE_WORDS // SLOTS].bitcast(U8),
+                rhs=ra_mx[g][0][:, assets].bitcast(FP8X4),
+                rhs_scale=ra_mx[g][1][:, assets],
+                start=(g == 0),
+                stop=(g == RA_PASSES - 1),
+            )
+
+        def u_passes(grp, t, first=0, stop=RA_PASSES):
+            if first == 0:
+                u_sums[t] = u_bank(t)
+            for g in range(first, stop):
+                u_matmul(u_sums[t][:], grp, t, g, slice(0, ASSETS))
+
+        def u_tile(grp, a):
+            u_sums[a] = u_bank(a)
+            for t in range(SLOTS):
+                for g in range(RA_PASSES):
+                    u_matmul(u_sums[a][:, t * P : (t + 1) * P], grp, t, g, slice(a * P, (a + 1) * P))
 
         def v_pass(grp, t, g):
             if g == 0:
@@ -169,6 +179,17 @@ def tile_clipped_overlap_covariance_s11_kernel(tc, ra, ovl_words, ovl_scales, wt
                 scale=per_interval[:, t, grp : grp + 1],
             )
 
+        def weigh_tile(grp, a):
+            if a == 0:
+                u_packed[grp] = new_packed()
+                u_mx[grp] = new_mx("u%d" % grp)
+            nc.vector.tensor_tensor(
+                out=u_packed[grp][:, a * K_PASS : (a + 1) * K_PASS].rearrange("p (i t) -> p i t", t=SLOTS),
+                in0=u_sums[a][:].rearrange("p (t i) -> p i t", t=SLOTS),
+                in1=per_interval[:, :, grp].unsqueeze(1).to_broadcast([P, P, SLOTS]),
+                op=mybir.AluOpType.mult,
+            )
+
         def clip(grp, t):
             if t == 0:
                 v_slots[grp] = sb.tile([P, SLOTS, ASSETS], BF16, name="v_slots%d" % grp)
@@ -189,14 +210,17 @@ def tile_clipped_overlap_covariance_s11_kernel(tc, ra, ovl_words, ovl_scales, wt
                 in_=slots[grp][:, :, first:stop].rearrange("p t (c i) -> p c t i", i=4),
             )
 
-        def pack_u(grp, copy, first=0, stop=ASSETS):
-            pack_slots(u_slots, u_packed, grp, copy, first, stop)
+        def pack_u(grp, copy):
+            pack_slots(u_slots, u_packed, grp, copy)
 
         def pack_v(grp, copy, first=0, stop=ASSETS):
             pack_slots(v_slots, v_packed, grp, copy, first, stop)
 
         def quantise_u(grp):
             u_mx[grp] = quantise(u_packed[grp], "u%d" % grp)
+
+        def quantise_u_tile(grp, a):
+            quantise_columns(u_mx[grp], u_packed[grp], a * P, (a + 1) * P)
 
         def quantise_v(grp):
             v_mx[grp] = quantise(v_packed[grp], "v%d" % grp)
@@ -305,16 +329,18 @@ def tile_clipped_overlap_covariance_s11_kernel(tc, ra, ovl_words, ovl_scales, wt
         pack_v(0, on_vector, ASSETS // 2, ASSETS)
         quantise_diff(1, 1)
         for t in range(2):
-            u_slot(0, t)
+            u_passes(0, t, 0, RA_PASSES - 1)
+        for t in range(2):
+            u_passes(0, t, RA_PASSES - 1, RA_PASSES)
             weigh(0, t)
         pack_diff(2, 0, on_scalar)
         sort_ovl_scales(1)
         sort_ovl_codes(1)
-        u_slot(0, 2)
+        u_passes(0, 2)
         for t in range(SLOTS):
             v_pass(1, t, 1)
             clip(1, t)
-        u_slot(0, 3)
+        u_passes(0, 3)
         for t in range(2, SLOTS):
             weigh(0, t)
 
@@ -322,42 +348,45 @@ def tile_clipped_overlap_covariance_s11_kernel(tc, ra, ovl_words, ovl_scales, wt
         scalar_packs = {
             1: [lambda: pack_diff(last, 0, on_scalar)],
             2: [lambda: pack_v(1, on_scalar), lambda: pack_u(0, on_scalar)],
-            3: [lambda: pack_u(1, on_scalar), lambda: pack_u(2, on_scalar)],
         }
-        for grp in range(1, GROUPS):
+        for grp in range(1, last):
             scalar_packs[grp][0]()
-            u_slot(grp, 0)
+            u_passes(grp, 0)
             weigh(grp, 0)
             for pack in scalar_packs[grp][1:]:
                 pack()
             for t in range(1, SLOTS):
-                u_slot(grp, t)
+                u_passes(grp, t)
                 weigh(grp, t)
-            if grp < last:
-                pack_diff(grp + 1, 1, on_vector)
-                for g in range(YB_PASSES):
-                    quantise_diff(grp + 1, g)
-                sort_ovl_scales(grp + 1)
-                sort_ovl_codes(grp + 1)
-                quantise_v(grp - 1)
-                for t in range(SLOTS):
-                    v_slot(grp + 1, t)
-                    clip(grp + 1, t)
+            pack_diff(grp + 1, 1, on_vector)
+            for g in range(YB_PASSES):
+                quantise_diff(grp + 1, g)
+            sort_ovl_scales(grp + 1)
+            sort_ovl_codes(grp + 1)
+            quantise_v(grp - 1)
+            for t in range(SLOTS):
+                v_slot(grp + 1, t)
+                clip(grp + 1, t)
 
+        for a in range(ASSET_TILES):
+            u_tile(last, a)
+        pack_u(1, on_scalar)
+        pack_u(2, on_scalar)
+        pack_v(last, on_scalar)
         quantise_u(0)
         pack_v(2, on_vector)
+        weigh_tile(last, 0)
         quantise_u(1)
-        pack_v(last, on_vector)
         quantise_v(2)
+        weigh_tile(last, 1)
+        quantise_u_tile(last, 0)
         quantise_u(2)
+        quantise_u_tile(last, 1)
+        weigh_tile(last, 2)
         quantise_v(last)
-        u_mx[last] = new_mx("u%d" % last)
-        for a in range(2):
-            pack_u(last, on_scalar, a * P, (a + 1) * P)
-        for a in range(ASSET_TILES):
-            quantise_columns(u_mx[last], u_packed[last], a * P, (a + 1) * P)
-            if a + 2 < ASSET_TILES:
-                pack_u(last, on_vector, (a + 2) * P, (a + 3) * P)
+        weigh_tile(last, 3)
+        quantise_u_tile(last, 2)
+        quantise_u_tile(last, 3)
 
         for grp in range(2):
             for a in range(ASSET_TILES):

from contextlib import ExitStack

import concourse.mybir as mybir
from concourse.masks import make_identity

ASSETS, TICKS_A, TICKS_B, INTERVALS = 512, 2048, 1024, 2048
FLOPS = 2 * ASSETS * (TICKS_A * INTERVALS + TICKS_B * INTERVALS + INTERVALS * ASSETS)

F32 = mybir.dt.float32
BF16 = mybir.dt.bfloat16
I32 = mybir.dt.int32
U8 = mybir.dt.uint8
FP8X4 = mybir.dt.float8_e4m3fn_x4
FP4X4 = mybir.dt.float4_e2m1fn_x4

P = 128
SLOTS = 4
K_PASS = P * SLOTS
RUN = 8
RA_PASSES, YB_PASSES, GROUPS = TICKS_A // K_PASS, TICKS_B // K_PASS, INTERVALS // K_PASS
ASSET_TILES = ASSETS // P
CODE_WORDS = K_PASS // 2
SCALE_WORDS = K_PASS // 4
PACKED_BUFS = 8


def tile_clipped_overlap_covariance_s11_kernel(tc, ra, ovl_words, ovl_scales, wt, yb, diff, lo, hi, out):
    nc = tc.nc
    on_vector, on_scalar = nc.vector.tensor_copy, nc.scalar.copy

    with ExitStack() as ctx:
        sb = ctx.enter_context(tc.tile_pool(name="sb", bufs=1))
        psum = ctx.enter_context(tc.psum_pool(name="psum", bufs=1))
        ctx.enter_context(tc.manual_schedule())

        def u_bank(n):
            return psum.tile([P, K_PASS], F32, name="u_bank%d" % n)

        def v_bank(n):
            return psum.tile([P, K_PASS], F32, name="v_bank%d" % n)

        def new_packed():
            return sb.tile([P, K_PASS * SLOTS], BF16, name="packed", bufs=PACKED_BUFS, align_bytes=64)

        def new_mx(name):
            codes = sb.tile([P, K_PASS], I32, name=name + "_codes", align_bytes=64)
            scales = sb.tile([P, K_PASS], U8, name=name + "_scales", align_bytes=64)
            return codes, scales

        def quantise_columns(mx, packed, first, stop):
            nc.vector.quantize_mx(
                out=mx[0][:, first:stop].bitcast(FP8X4),
                scales=mx[1][:, first:stop],
                in_=packed[:, SLOTS * first : SLOTS * stop],
            )

        def quantise(packed, name):
            mx = new_mx(name)
            quantise_columns(mx, packed, 0, K_PASS)
            return mx

        tick_words, tick_packed = {}, {}

        def load_ticks(name, src, first_pass, half):
            rows = sb.tile([P, 2, 2 * K_PASS], BF16, name="%s_rows%d_%d" % (name, first_pass, half))
            part = src[half * 2 * P : (half + 1) * 2 * P, first_pass * K_PASS : (first_pass + 2) * K_PASS]
            nc.sync.dma_start(out=rows[:], in_=part.rearrange("(a p) k -> p a k", p=P))
            for g in range(2):
                tick_words[name, first_pass + g, half] = rows[:].bitcast(F32)[:, :, g * 2 * P : (g + 1) * 2 * P]

        def turn_ticks(name, g, half, copy):
            if half == 0:
                tick_packed[name, g] = new_packed()
            bank = u_bank(2 * half + g % 2)
            for a in range(2):
                for u in range(2):
                    column = (2 * a + u) * P
                    nc.tensor.transpose(bank[:, column : column + P], tick_words[name, g, half][:, a, u : 2 * P : 2], ident[:])
            words = tick_packed[name, g][:].bitcast(F32)[:, half * K_PASS : (half + 1) * K_PASS]
            copy(out=words.rearrange("p (a i u) -> p a i u", a=2, u=2), in_=bank[:].rearrange("p (a u i) -> p a i u", a=2, u=2))

        diff_rows, diff_packed, diff_mx = {}, {}, {}

        def load_diff(grp, g):
            rows = sb.tile([P, SLOTS, K_PASS], BF16, name="diff_rows%d_%d" % (grp, g))
            part = diff[g * K_PASS : (g + 1) * K_PASS, grp * K_PASS : (grp + 1) * K_PASS]
            nc.sync.dma_start(out=rows[:], in_=part.rearrange("(p j) l -> p j l", j=SLOTS))
            diff_rows[grp, g] = rows

        def pack_diff(grp, g, copy, first=0, stop=SLOTS):
            if first == 0:
                diff_packed[grp, g] = new_packed()
            copy(
                out=diff_packed[grp, g][:].rearrange("p (t q r j) -> p q t j r", t=SLOTS, r=RUN, j=SLOTS)[:, :, first:stop],
                in_=diff_rows[grp, g][:].rearrange("p j (q t r) -> p q t j r", t=SLOTS, r=RUN)[:, :, first:stop],
            )

        def quantise_diff(grp, g):
            diff_mx[grp, g] = quantise(diff_packed[grp, g], "diff%d_%d" % (grp, g))

        ovl_rows, ovl_codes, ovl_planes = {}, {}, {}

        def load_ovl(grp):
            words = sb.tile([P, RA_PASSES, CODE_WORDS], I32, name="ovl_rows%d" % grp)
            part = ovl_words.bitcast(I32)[:, :, grp * CODE_WORDS : (grp + 1) * CODE_WORDS]
            nc.sync.dma_start(out=words[:], in_=part.rearrange("g p w -> p g w"))
            ovl_rows[grp] = words

        def load_ovl_scales(rows, first_grp, stop_grp):
            part = ovl_scales.bitcast(I32)[:, :, first_grp * SCALE_WORDS : stop_grp * SCALE_WORDS]
            for r in range(4):
                nc.sync.dma_start(out=rows[r:P:32, :, :], in_=part[:, r:16:4, :].rearrange("g q w -> q g w"))

        def sort_by_slot(src, words, name):
            dst = sb.tile([P, RA_PASSES, words], I32, name=name, align_bytes=64)
            run = words * RUN // K_PASS
            nc.vector.tensor_copy(
                out=dst[:].rearrange("p g (t q w) -> p g t q w", t=SLOTS, w=run),
                in_=src.rearrange("p g (q t w) -> p g t q w", t=SLOTS, w=run),
            )
            return dst

        def sort_ovl_scales(grp):
            ovl_planes[grp] = sort_by_slot(scale_rows[grp], SCALE_WORDS, "ovl_plane%d" % grp)

        def sort_ovl_codes(grp):
            ovl_codes[grp] = sort_by_slot(ovl_rows[grp][:], CODE_WORDS, "ovl_codes%d" % grp)

        ra_mx, yb_mx, u_mx, v_mx = {}, {}, {}, {}
        u_sums, v_sums, u_slots, v_slots, u_packed, v_packed = {}, {}, {}, {}, {}, {}

        def u_matmul(sums, grp, t, g, assets):
            nc.tensor.matmul_mx(
                out=sums,
                lhsT=ovl_codes[grp][:, g, t * CODE_WORDS // SLOTS : (t + 1) * CODE_WORDS // SLOTS].bitcast(FP4X4),
                lhsT_scale=ovl_planes[grp][:, g, t * SCALE_WORDS // SLOTS : (t + 1) * SCALE_WORDS // SLOTS].bitcast(U8),
                rhs=ra_mx[g][0][:, assets].bitcast(FP8X4),
                rhs_scale=ra_mx[g][1][:, assets],
                start=(g == 0),
                stop=(g == RA_PASSES - 1),
            )

        def u_passes(grp, t, first=0, stop=RA_PASSES):
            if first == 0:
                u_sums[t] = u_bank(t)
            for g in range(first, stop):
                u_matmul(u_sums[t][:], grp, t, g, slice(0, ASSETS))

        def u_tile(grp, a):
            u_sums[a] = u_bank(a)
            for t in range(SLOTS):
                for g in range(RA_PASSES):
                    u_matmul(u_sums[a][:, t * P : (t + 1) * P], grp, t, g, slice(a * P, (a + 1) * P))

        def v_pass(grp, t, g):
            if g == 0:
                v_sums[t] = v_bank(t)
            nc.tensor.matmul_mx(
                out=v_sums[t][:],
                lhsT=diff_mx[grp, g][0][:, t * P : (t + 1) * P].bitcast(FP8X4),
                lhsT_scale=diff_mx[grp, g][1][:, t * P : (t + 1) * P],
                rhs=yb_mx[g][0][:].bitcast(FP8X4),
                rhs_scale=yb_mx[g][1][:],
                start=(g == 0),
                stop=(g == YB_PASSES - 1),
            )

        def v_slot(grp, t):
            for g in range(YB_PASSES):
                v_pass(grp, t, g)

        def weigh(grp, t):
            if t == 0:
                u_slots[grp] = sb.tile([P, SLOTS, ASSETS], BF16, name="u_slots%d" % grp)
            nc.scalar.activation(
                out=u_slots[grp][:, t, :],
                in_=u_sums[t][:],
                func=mybir.ActivationFunctionType.Copy,
                scale=per_interval[:, t, grp : grp + 1],
            )

        def weigh_tile(grp, a):
            if a == 0:
                u_packed[grp] = new_packed()
                u_mx[grp] = new_mx("u%d" % grp)
            nc.vector.tensor_tensor(
                out=u_packed[grp][:, a * K_PASS : (a + 1) * K_PASS].rearrange("p (i t) -> p i t", t=SLOTS),
                in0=u_sums[a][:].rearrange("p (t i) -> p i t", t=SLOTS),
                in1=per_interval[:, :, grp].unsqueeze(1).to_broadcast([P, P, SLOTS]),
                op=mybir.AluOpType.mult,
            )

        def clip(grp, t):
            if t == 0:
                v_slots[grp] = sb.tile([P, SLOTS, ASSETS], BF16, name="v_slots%d" % grp)
            nc.vector.tensor_scalar(
                out=v_slots[grp][:, t, :],
                in0=v_sums[t][:],
                scalar1=per_interval[:, t, GROUPS + grp : GROUPS + grp + 1],
                scalar2=per_interval[:, t, 2 * GROUPS + grp : 2 * GROUPS + grp + 1],
                op0=mybir.AluOpType.max,
                op1=mybir.AluOpType.min,
            )

        def pack_slots(slots, packed, grp, copy, first=0, stop=ASSETS):
            if first == 0:
                packed[grp] = new_packed()
            copy(
                out=packed[grp][:, SLOTS * first : SLOTS * stop].rearrange("p (c i t) -> p c t i", i=4, t=SLOTS),
                in_=slots[grp][:, :, first:stop].rearrange("p t (c i) -> p c t i", i=4),
            )

        def pack_u(grp, copy):
            pack_slots(u_slots, u_packed, grp, copy)

        def pack_v(grp, copy, first=0, stop=ASSETS):
            pack_slots(v_slots, v_packed, grp, copy, first, stop)

        def quantise_u(grp):
            u_mx[grp] = quantise(u_packed[grp], "u%d" % grp)

        def quantise_u_tile(grp, a):
            quantise_columns(u_mx[grp], u_packed[grp], a * P, (a + 1) * P)

        def quantise_v(grp):
            v_mx[grp] = quantise(v_packed[grp], "v%d" % grp)

        out_sums = {}

        def out_pass(a, grp):
            if grp == 0:
                out_sums[a] = v_bank(a)
            nc.tensor.matmul_mx(
                out=out_sums[a][:],
                lhsT=u_mx[grp][0][:, a * P : (a + 1) * P].bitcast(FP8X4),
                lhsT_scale=u_mx[grp][1][:, a * P : (a + 1) * P],
                rhs=v_mx[grp][0][:].bitcast(FP8X4),
                rhs_scale=v_mx[grp][1][:],
                start=(grp == 0),
                stop=(grp == GROUPS - 1),
            )

        def store(a):
            result = sb.tile([P, ASSETS], F32, name="result%d" % a)
            nc.scalar.copy(out=result[:], in_=out_sums[a][:])
            nc.sync.dma_start(out=out[a * P : (a + 1) * P, :], in_=result[:])

        ident = sb.tile([P, P], F32, name="ident")
        make_identity(nc, ident[:])
        vector_count = 3 * GROUPS
        vector_rows = sb.tile([P, K_PASS], BF16, name="vector_rows")
        vector_sorted = sb.tile([P, K_PASS], F32, name="vector_sorted")
        per_interval = sb.tile([P, SLOTS, vector_count], F32, name="per_interval")
        nc.gpsimd.memset(vector_sorted[:], 0.0)
        scale_tiles = [sb.tile([P, RA_PASSES, n * SCALE_WORDS], I32, name="scale_rows%d" % i) for i, n in enumerate((1, 1, 2))]
        for zeroed in scale_tiles:
            nc.vector.memset(zeroed[:], 0)
        scale_rows = [scale_tiles[0][:], scale_tiles[1][:], scale_tiles[2][:, :, 0:SCALE_WORDS], scale_tiles[2][:, :, SCALE_WORDS:]]

        for half in range(2):
            load_ticks("yb", yb, 0, half)
        for n, vec in enumerate((wt, lo, hi)):
            nc.sync.dma_start(out=vector_rows[n * GROUPS : (n + 1) * GROUPS, :], in_=vec.rearrange("(g l) -> g l", g=GROUPS))
        load_diff(0, 0)
        load_diff(0, 1)
        for half in range(2):
            load_ticks("ra", ra, 0, half)
        load_diff(1, 0)
        for half in range(2):
            load_ticks("ra", ra, 2, half)
        load_ovl_scales(scale_tiles[0], 0, 1)
        load_ovl(0)
        load_diff(1, 1)
        load_diff(2, 0)
        load_ovl_scales(scale_tiles[1], 1, 2)
        load_ovl(1)
        load_diff(2, 1)
        load_diff(3, 0)
        load_ovl_scales(scale_tiles[2], 2, GROUPS)
        load_ovl(2)
        load_diff(3, 1)
        load_ovl(3)

        for half in range(2):
            for g in range(YB_PASSES):
                turn_ticks("yb", g, half, on_scalar)
        nc.vector.tensor_copy(
            out=vector_sorted[0:vector_count, :].rearrange("p (t q r) -> p t q r", t=SLOTS, r=RUN),
            in_=vector_rows[0:vector_count, :].rearrange("p (q t r) -> p t q r", t=SLOTS, r=RUN),
        )
        vector_bank = v_bank(SLOTS - 1)
        for t in range(SLOTS):
            nc.tensor.transpose(vector_bank[:, t * P : (t + 1) * P], vector_sorted[:, t * P : (t + 1) * P], ident[:])
        nc.scalar.copy(out=per_interval[:], in_=vector_bank[:].rearrange("p (t c) -> p t c", t=SLOTS)[:, :, 0:vector_count])
        pack_diff(0, 0, on_vector)
        for g in range(YB_PASSES):
            yb_mx[g] = quantise(tick_packed["yb", g], "yb%d" % g)
        pack_diff(0, 1, on_scalar)
        quantise_diff(0, 0)

        for g in range(2):
            turn_ticks("ra", g, 0, on_vector)
        quantise_diff(0, 1)
        for g in range(2):
            turn_ticks("ra", g, 1, on_scalar)
        ra_mx[0] = quantise(tick_packed["ra", 0], "ra0")
        for t in range(SLOTS - 1):
            v_slot(0, t)
            clip(0, t)
        pack_diff(1, 0, on_scalar)
        for g in range(2, RA_PASSES):
            turn_ticks("ra", g, 0, on_scalar)
        v_slot(0, SLOTS - 1)
        ra_mx[1] = quantise(tick_packed["ra", 1], "ra1")
        quantise_diff(1, 0)
        sort_ovl_scales(0)
        clip(0, SLOTS - 1)
        for g in range(2, RA_PASSES):
            turn_ticks("ra", g, 1, on_scalar)
        for t in range(SLOTS):
            v_pass(1, t, 0)
        sort_ovl_codes(0)
        for g in range(2, RA_PASSES):
            ra_mx[g] = quantise(tick_packed["ra", g], "ra%d" % g)

        pack_v(0, on_scalar, 0, ASSETS // 2)
        pack_diff(1, 1, on_vector, 0, SLOTS // 2)
        pack_diff(1, 1, on_scalar, SLOTS // 2, SLOTS)
        pack_v(0, on_vector, ASSETS // 2, ASSETS)
        quantise_diff(1, 1)
        for t in range(2):
            u_passes(0, t, 0, RA_PASSES - 1)
        for t in range(2):
            u_passes(0, t, RA_PASSES - 1, RA_PASSES)
            weigh(0, t)
        pack_diff(2, 0, on_scalar)
        sort_ovl_scales(1)
        sort_ovl_codes(1)
        u_passes(0, 2)
        for t in range(SLOTS):
            v_pass(1, t, 1)
            clip(1, t)
        u_passes(0, 3)
        for t in range(2, SLOTS):
            weigh(0, t)

        last = GROUPS - 1
        scalar_packs = {
            1: [lambda: pack_diff(last, 0, on_scalar)],
            2: [lambda: pack_v(1, on_scalar), lambda: pack_u(0, on_scalar)],
        }
        for grp in range(1, last):
            scalar_packs[grp][0]()
            u_passes(grp, 0)
            weigh(grp, 0)
            for pack in scalar_packs[grp][1:]:
                pack()
            for t in range(1, SLOTS):
                u_passes(grp, t)
                weigh(grp, t)
            pack_diff(grp + 1, 1, on_vector)
            for g in range(YB_PASSES):
                quantise_diff(grp + 1, g)
            sort_ovl_scales(grp + 1)
            sort_ovl_codes(grp + 1)
            quantise_v(grp - 1)
            for t in range(SLOTS):
                v_slot(grp + 1, t)
                clip(grp + 1, t)

        for a in range(ASSET_TILES):
            u_tile(last, a)
        pack_u(1, on_scalar)
        pack_u(2, on_scalar)
        pack_v(last, on_scalar)
        quantise_u(0)
        pack_v(2, on_vector)
        weigh_tile(last, 0)
        quantise_u(1)
        quantise_v(2)
        weigh_tile(last, 1)
        quantise_u_tile(last, 0)
        quantise_u(2)
        quantise_u_tile(last, 1)
        weigh_tile(last, 2)
        quantise_v(last)
        weigh_tile(last, 3)
        quantise_u_tile(last, 2)
        quantise_u_tile(last, 3)

        for grp in range(2):
            for a in range(ASSET_TILES):
                out_pass(a, grp)
        for a in range(ASSET_TILES):
            for grp in range(2, GROUPS):
                out_pass(a, grp)
            store(a)
